import numpy as np
import ml_dtypes


def mxq(x, axis, fmt="e4m3"):
    dtype, down = {"e4m3": (ml_dtypes.float8_e4m3fn, 7), "e5m2": (ml_dtypes.float8_e5m2, 14)}[fmt]
    v = np.moveaxis(np.asarray(x, np.float32).astype(ml_dtypes.bfloat16).astype(np.float64), axis, -1)
    blocks = v.reshape(v.shape[:-1] + (-1, 32))
    amax = np.abs(blocks).max(-1, keepdims=True)
    byte = np.maximum(np.where(amax > 0, np.frexp(amax)[1] - 1 + 127, 0) - down, 1)
    scale = np.exp2(byte - 127.0)
    codes = (blocks / scale).astype(np.float32).astype(dtype).astype(np.float64)
    return np.moveaxis((codes * scale).reshape(v.shape), -1, axis)


WIDE = False


def mx_kscale(k):
    if not WIDE:
        return np.ones(k)
    levels = np.array([10, -10, 5, -5, 0])
    if k % 512:
        return np.exp2(np.random.permutation(np.resize(levels, k // 32))).repeat(32)
    a = np.empty((k // 512, 16))
    for p in range(k // 512):
        a[p, :8] = np.random.permutation(np.resize(levels, 8))
        for g in range(8):
            far = levels[np.abs(levels - a[p, g]) >= 10]
            a[p, g + 8] = far[np.random.randint(len(far))]
    return np.exp2(a.ravel()).repeat(32)


def f64(x):
    return np.asarray(x).astype(np.float64)


def striped(idx):
    return np.tile(idx.reshape(-1, 16).T, (8, 1)).astype(np.uint16)


def unstriped(offs):
    return offs[:16].T.reshape(-1).astype(np.int64)


E2M1 = np.array([0.0, 0.5, 1.0, 1.5, 2.0, 3.0, 4.0, 6.0, -0.0, -0.5, -1.0, -1.5, -2.0, -3.0, -4.0, -6.0])


def pack_weight(w, fmt):
    k, n = w.shape
    w = f64(np.asarray(w, np.float32).astype(ml_dtypes.bfloat16)).reshape(k // 32, 32, n)
    amax = np.abs(w).max(1)
    if fmt == "e4m3":
        byte = np.frexp(amax)[1] - 1 + 127 - 7
    else:
        mant, ex = np.frexp(amax / 6.0)
        byte = np.where(mant > 0.5, ex, ex - 1) + 127
    byte = np.clip(np.where(amax > 0, byte, 1), 1, 254)
    scaled = (w * np.exp2(127.0 - byte)[:, None, :]).reshape(k, n).astype(np.float32)
    by_word = np.ascontiguousarray(scaled.reshape(k // 512, 128, 4, n).transpose(0, 1, 3, 2))
    if fmt == "e4m3":
        words = by_word.astype(ml_dtypes.float8_e4m3fn).view(np.uint8)
    else:
        c = by_word.astype(ml_dtypes.float4_e2m1fn).view(np.uint8) & 0xF
        words = (c[..., 0::2] | (c[..., 1::2] << 4)).reshape(k // 512, 128, 2 * n)
    return np.ascontiguousarray(words), np.ascontiguousarray(byte.astype(np.uint8).reshape(k // 512, 16, n))


def unpack_weight(words, scales, fmt):
    g, _, n = scales.shape
    words = np.ascontiguousarray(words).reshape(g, 128, n, -1)
    if fmt == "e4m3":
        vals = words.view(ml_dtypes.float8_e4m3fn).astype(np.float64)
    else:
        nib = np.empty((g, 128, n, 4), np.uint8)
        nib[..., 0::2] = words & 0xF
        nib[..., 1::2] = words >> 4
        vals = E2M1[nib]
    vals = vals * np.repeat(np.exp2(scales.astype(np.float64) - 127.0), 8, axis=1)[..., None]
    return vals.transpose(0, 1, 3, 2).reshape(g * 512, n)


def gelu(v):
    return 0.5 * v * (1.0 + np.tanh(np.sqrt(2.0 / np.pi) * (v + 0.044715 * v**3)))


K, T, S, T2, S2, N = 1024, 4096, 1024, 2048, 1024, 512


def setup_inputs():
    n = np.random.standard_normal
    s = mx_kscale(K)[:, None]
    u = mx_kscale(S)[:, None]
    tab_words, tab_scales = pack_weight(n((K, T)) * s * (0.6 / np.sqrt(K)), "e4m3")
    tab2_words, tab2_scales = pack_weight(n((K, T2)) / s, "e4m3")
    w4_words, w4_scales = pack_weight(n((S, N)) / np.sqrt(S) / u, "e2m1")
    wg = (n((S, N)) / np.sqrt(S) / u).astype(np.float32)
    dec = (np.exp(-1.5 * np.random.rand(S)) * u[:, 0]).astype(np.float32)
    offs = striped(np.random.permutation(T)[:S])
    offs2 = striped(np.random.permutation(T2)[:S2])
    return {"tab_words": tab_words, "tab_scales": tab_scales,
            "tab2_words": tab2_words, "tab2_scales": tab2_scales,
            "w4_words": w4_words, "w4_scales": w4_scales,
            "wg": wg, "dec": dec, "offs": offs, "offs2": offs2}


def reference(tab_words, tab_scales, tab2_words, tab2_scales, w4_words, w4_scales, wg, dec, offs, offs2):
    v = unpack_weight(tab_words, tab_scales, "e4m3")[:, unstriped(offs)]
    v2 = unpack_weight(tab2_words, tab2_scales, "e4m3")[:, unstriped(offs2)]
    a = v.T @ v2
    p = np.exp(a) * f64(dec)[:, None]
    pq = mxq(p, 0, "e4m3")
    y = unpack_weight(w4_words, w4_scales, "e2m1").T @ pq
    g = mxq(f64(wg), 0, "e4m3").T @ pq
    out = y * (1.0 / (1.0 + np.exp(-g)))
    return out

@@ -1,0 +1,246 @@
+from contextlib import ExitStack
+
+import concourse.mybir as mybir
+
+K, T, S, T2, S2, N = 1024, 4096, 1024, 2048, 1024, 512
+FLOPS = 2 * K * S * S2 + 2 * 2 * S * N * S2
+
+F32 = mybir.dt.float32
+BF16 = mybir.dt.bfloat16
+I32 = mybir.dt.int32
+U32 = mybir.dt.uint32
+U16 = mybir.dt.uint16
+U8 = mybir.dt.uint8
+FP8X4 = mybir.dt.float8_e4m3fn_x4
+FP4X4 = mybir.dt.float4_e2m1fn_x4
+ACT = mybir.ActivationFunctionType
+ALU = mybir.AluOpType
+
+P = 128
+PACK = 4
+PASS = P * PACK
+BANK = 512
+KEY_ROW = (0, 4)
+QUERY_ROW = (8, 12)
+
+
+def tile_list_decayed_key_read_kernel(
+    tc, tab_words, tab_scales, tab2_words, tab2_scales, w4_words, w4_scales, wg, dec, offs, offs2, out
+):
+    nc = tc.nc
+    with ExitStack() as ctx:
+        lists = ctx.enter_context(tc.tile_pool(name="lists", bufs=1))
+        keep = ctx.enter_context(tc.tile_pool(name="keep", bufs=1))
+        ring = ctx.enter_context(tc.tile_pool(name="ring", bufs=4))
+        tail = ctx.enter_context(tc.tile_pool(name="tail", bufs=4))
+        psum = ctx.enter_context(tc.psum_pool(name="psum", bufs=1))
+
+        key_list = lists.tile([P, S // 16], U16, name="key_list")
+        query_list = lists.tile([P, S2 // 16], U16, name="query_list")
+
+        key_table = [keep.tile([P, T], I32, name="key_table%d" % a, align_bytes=64) for a in range(2)]
+        query_table = [keep.tile([P, T2], I32, name="query_table%d" % a, tag="query_table%d" % a, align_bytes=64) for a in range(2)]
+        key_scale_table = keep.tile([P, T // 4], I32, name="key_scale_table", tag="slot_b", align_bytes=64)
+        query_scale_table = keep.tile([P, T2 // 4], I32, name="query_scale_table", tag="slot_a", align_bytes=64)
+        w4_codes = keep.tile([P, 2, N // 2], I32, name="w4_codes", align_bytes=64)
+        w4_plane = keep.tile([P, 2, N // 4], I32, name="w4_plane", align_bytes=64)
+        wg_raw = [keep.tile([P, PACK, N], F32, name="wg_raw%d" % b, align_bytes=64) for b in range(2)]
+        decay = keep.tile([P, 2, PACK], F32, name="decay")
+        log_decay = keep.tile([P, 2, PACK], F32, name="log_decay")
+
+        nc.vector.memset(query_scale_table[:], 0)
+        nc.vector.memset(key_scale_table[:], 0)
+        nc.vector.memset(w4_plane[:], 0)
+
+        def load_words(tile, words):
+            nc.sync.dma_start(out=tile[:], in_=words.rearrange("p t i -> p (t i)").bitcast(I32))
+
+        nc.sync.dma_start(query_list[:], offs2)
+        load_words(query_table[0], tab2_words[0])
+        nc.sync.dma_start(key_list[:], offs)
+        load_words(key_table[0], tab_words[0])
+        nc.sync.dma_start(out=decay[:], in_=dec.rearrange("(b p t) -> p b t", b=2, t=PACK))
+        load_words(key_table[1], tab_words[1])
+        load_words(query_table[1], tab2_words[1])
+        for b in range(2):
+            nc.sync.dma_start(
+                out=wg_raw[b][:], in_=wg[b * PASS : (b + 1) * PASS, :].rearrange("(p t) n -> p t n", t=PACK)
+            )
+        nc.sync.dma_start(out=w4_codes[:], in_=w4_words.bitcast(I32).rearrange("a p c -> p a c"))
+
+        for tile, scales, row in ((query_scale_table, tab2_scales, QUERY_ROW[0]), (key_scale_table, tab_scales, KEY_ROW[0])):
+            for q in range(4):
+                nc.gpsimd.dma_start(
+                    out=tile[32 * q + row : 32 * q + row + 8, :], in_=scales.bitcast(I32)[:, 4 * q : 4 * q + 4, :]
+                )
+        for q in range(4):
+            nc.sync.dma_start(
+                out=w4_plane[32 * q : 32 * q + 4, :, :],
+                in_=w4_scales.bitcast(I32)[:, 4 * q : 4 * q + 4, :].rearrange("a r n -> r a n"),
+            )
+
+        nc.scalar.activation(out=log_decay[:], in_=decay[:], func=ACT.Ln, scale=0.5)
+        warm = keep.tile([P, 1], F32, name="warm")
+        nc.scalar.activation(out=warm[:], in_=log_decay[:, 0, 0:1], func=ACT.Exp)
+
+        keys = {}
+        queries = {0: keep.tile([P, S2], U32, name="queries0", align_bytes=64)}
+        key_plane_listed = keep.tile([P, S], U8, name="key_plane_listed", tag="slot_c", align_bytes=64)
+        key_plane = keep.tile([P, S], U8, name="key_plane", align_bytes=64)
+        query_plane = keep.tile([P, S2], U8, name="query_plane", align_bytes=64)
+
+        def half(h):
+            return slice(h * BANK, (h + 1) * BANK)
+
+        def list_half(tile, h):
+            return tile[:, h * (BANK // 16) : (h + 1) * (BANK // 16)]
+
+        def gather_queries(a, h):
+            nc.vector.tensor_copy(
+                queries[a][:, half(h)], query_table[a][:].bitcast(U32).indirect(list_half(query_list, h))
+            )
+
+        def gather_keys(a, b):
+            nc.vector.tensor_copy(
+                keys[a][:, half(b)].rearrange("p (t m) -> p m t", t=PACK),
+                key_table[a][:].bitcast(U32).indirect(list_half(key_list, b)),
+            )
+
+        for h in range(2):
+            gather_queries(0, h)
+        for h in range(2):
+            nc.vector.tensor_copy(
+                query_plane[:, half(h)], query_scale_table[:].bitcast(U8).indirect(list_half(query_list, h))
+            )
+        keys[0] = keep.tile([P, S], U32, name="keys0", tag="slot_a", align_bytes=64)
+        for b in range(2):
+            gather_keys(0, b)
+        for b in range(2):
+            nc.vector.tensor_copy(
+                key_plane_listed[:, half(b)], key_scale_table[:].bitcast(U8).indirect(list_half(key_list, b))
+            )
+        nc.vector.tensor_copy(
+            key_plane[:].rearrange("p (b t m) -> p b t m", b=2, t=PACK),
+            key_plane_listed[:].rearrange("p (b m t) -> p b t m", b=2, t=PACK),
+        )
+
+        def bank(n):
+            return psum.tile([P, BANK], F32, name="bank%d" % n)
+
+        def score_pass(acc, a, tile_index, h):
+            cols = slice(tile_index * P, (tile_index + 1) * P)
+            nc.tensor.matmul_mx(
+                out=acc[:],
+                lhsT=keys[a][:, cols].bitcast(FP8X4),
+                lhsT_scale=key_plane[KEY_ROW[a] : P, cols],
+                rhs=queries[a][:, half(h)].bitcast(FP8X4),
+                rhs_scale=query_plane[QUERY_ROW[a] : P, half(h)],
+                start=(a == 0),
+                stop=(a == 1),
+            )
+
+        def interleave(dst, src):
+            nc.vector.tensor_copy(
+                out=dst[:].rearrange("p (c i) t -> p c t i", i=4), in_=src[:].rearrange("p t (c i) -> p c t i", i=4)
+            )
+
+        def quantize(codes, plane, grouped):
+            nc.vector.quantize_mx(
+                out=codes.bitcast(FP8X4), scales=plane, in_=grouped[:].rearrange("p n t -> p (n t)")
+            )
+
+        wg_codes = keep.tile([P, 2, N], U32, name="wg_codes", align_bytes=64)
+        wg_plane = keep.tile([P, 2, N], U8, name="wg_plane", align_bytes=64)
+        p_codes = [keep.tile([P, 2, BANK], U32, name="p_codes%d" % h, align_bytes=64) for h in range(2)]
+        p_plane = [keep.tile([P, 2, BANK], U8, name="p_plane%d" % h, align_bytes=64) for h in range(2)]
+
+        scores = [bank(n) for n in range(8)]
+        for n in range(8):
+            score_pass(scores[n], 0, n, 0)
+        keys[1] = keep.tile([P, S], U32, name="keys1", tag="slot_b", align_bytes=64)
+        for b in range(2):
+            gather_keys(1, b)
+        queries[1] = keep.tile([P, S2], U32, name="queries1", tag="slot_c", align_bytes=64)
+        for h in range(2):
+            gather_queries(1, h)
+
+        def exponentials(accs, b):
+            rows = ring.tile([P, PACK, BANK], BF16, name="rows", align_bytes=64)
+            for t in range(PACK):
+                nc.scalar.activation(
+                    out=rows[:, t, :], in_=accs[PACK * b + t][:], func=ACT.Exp, bias=log_decay[:, b, t : t + 1]
+                )
+            return rows
+
+        def pack_rows(rows):
+            grouped = ring.tile([P, BANK, PACK], BF16, name="grouped", align_bytes=64)
+            interleave(grouped, rows)
+            return grouped
+
+        for n in range(8):
+            score_pass(scores[n], 1, n, 0)
+        rows = {}
+        for b in range(2):
+            rows[0, b] = exponentials(scores, b)
+        wg_grouped = keep.tile([P, N, PACK], BF16, name="wg_grouped0", tag="query_table1", align_bytes=64)
+        interleave(wg_grouped, wg_raw[0])
+        grouped = pack_rows(rows[0, 0])
+        quantize(wg_codes[:, 0, :], wg_plane[:, 0, :], wg_grouped)
+        quantize(p_codes[0][:, 0, :], p_plane[0][:, 0, :], grouped)
+
+        scores = [bank(n) for n in range(8)]
+        for n in range(8):
+            for a in range(2):
+                score_pass(scores[n], a, n, 1)
+        for b in range(2):
+            rows[1, b] = exponentials(scores, b)
+        wg_grouped = pack_rows(wg_raw[1])
+        grouped = pack_rows(rows[0, 1])
+        quantize(wg_codes[:, 1, :], wg_plane[:, 1, :], wg_grouped)
+        quantize(p_codes[0][:, 1, :], p_plane[0][:, 1, :], grouped)
+
+        def read_pass(gate, value, n, h, b):
+            cols = slice(n * P, (n + 1) * P)
+            nc.tensor.matmul_mx(
+                out=gate[:],
+                lhsT=wg_codes[:, b, cols].bitcast(FP8X4),
+                lhsT_scale=wg_plane[:, b, cols],
+                rhs=p_codes[h][:, b, :].bitcast(FP8X4),
+                rhs_scale=p_plane[h][:, b, :],
+                start=(b == 0),
+                stop=(b == 1),
+            )
+            nc.tensor.matmul_mx(
+                out=value[:],
+                lhsT=w4_codes[:, b, n * (P // 2) : (n + 1) * (P // 2)].bitcast(FP4X4),
+                lhsT_scale=w4_plane[:, b, :].bitcast(U8)[:, cols],
+                rhs=p_codes[h][:, b, :].bitcast(FP8X4),
+                rhs_scale=p_plane[h][:, b, :],
+                start=(b == 0),
+                stop=(b == 1),
+            )
+
+        def finish(gate, value, n, h):
+            damp = tail.tile([P, BANK], F32, name="damp")
+            nc.scalar.activation(out=damp[:], in_=gate[:], func=ACT.Tanh)
+            result = tail.tile([P, BANK], F32, name="result")
+            nc.vector.scalar_tensor_tensor(
+                out=result[:], in0=damp[:], scalar=1.0, in1=value[:], op0=ALU.add, op1=ALU.mult
+            )
+            nc.sync.dma_start(out=out[n * P : (n + 1) * P, half(h)], in_=result[:])
+
+        reads = [bank(n) for n in range(8)]
+        for n in range(4):
+            for b in range(2):
+                read_pass(reads[2 * n], reads[2 * n + 1], n, 0, b)
+        both = [pack_rows(rows[1, b]) for b in range(2)]
+        for b in range(2):
+            quantize(p_codes[1][:, b, :], p_plane[1][:, b, :], both[b])
+        for n in range(4):
+            finish(reads[2 * n], reads[2 * n + 1], n, 0)
+        reads = [bank(n) for n in range(8)]
+        for n in range(4):
+            for b in range(2):
+                read_pass(reads[2 * n], reads[2 * n + 1], n, 1, b)
+        for n in range(4):
+            finish(reads[2 * n], reads[2 * n + 1], n, 1)

@@ -38,7 +38,7 @@ def tile_list_decayed_key_read_kernel(
         key_list = lists.tile([P, S // 16], U16, name="key_list")
         query_list = lists.tile([P, S2 // 16], U16, name="query_list")
 
-        key_table = [keep.tile([P, T], I32, name="key_table%d" % a, align_bytes=64) for a in range(2)]
+        key_table = [keep.tile([P, T], I32, name="key_table%d" % a, tag="key_table%d" % a, align_bytes=64) for a in range(2)]
         query_table = [keep.tile([P, T2], I32, name="query_table%d" % a, tag="query_table%d" % a, align_bytes=64) for a in range(2)]
         key_scale_table = keep.tile([P, T // 4], I32, name="key_scale_table", tag="slot_b", align_bytes=64)
         query_scale_table = keep.tile([P, T2 // 4], I32, name="query_scale_table", tag="slot_a", align_bytes=64)
@@ -49,43 +49,45 @@ def tile_list_decayed_key_read_kernel(
         log_decay = keep.tile([P, 2, PACK], F32, name="log_decay")
 
         nc.vector.memset(query_scale_table[:], 0)
-        nc.vector.memset(key_scale_table[:], 0)
+        nc.gpsimd.memset(key_scale_table[:], 0)
         nc.vector.memset(w4_plane[:], 0)
 
         def load_words(tile, words):
             nc.sync.dma_start(out=tile[:], in_=words.rearrange("p t i -> p (t i)").bitcast(I32))
 
+        def load_scale_rows(queue, tile, scales, row):
+            for q in range(4):
+                queue.dma_start(
+                    out=tile[32 * q + row : 32 * q + row + 8, :], in_=scales.bitcast(I32)[:, 4 * q : 4 * q + 4, :]
+                )
+
+        load_scale_rows(nc.gpsimd, key_scale_table, tab_scales, KEY_ROW[0])
         nc.sync.dma_start(query_list[:], offs2)
         load_words(query_table[0], tab2_words[0])
-        nc.sync.dma_start(key_list[:], offs)
-        load_words(key_table[0], tab_words[0])
-        nc.sync.dma_start(out=decay[:], in_=dec.rearrange("(b p t) -> p b t", b=2, t=PACK))
-        load_words(key_table[1], tab_words[1])
         load_words(query_table[1], tab2_words[1])
+        nc.sync.dma_start(key_list[:], offs)
+        nc.sync.dma_start(out=decay[:], in_=dec.rearrange("(b p t) -> p b t", b=2, t=PACK))
+        load_scale_rows(nc.sync, query_scale_table, tab2_scales, QUERY_ROW[0])
+        load_words(key_table[0], tab_words[0])
+        for q in range(4):
+            nc.sync.dma_start(
+                out=w4_plane[32 * q : 32 * q + 4, :, :],
+                in_=w4_scales.bitcast(I32)[:, 4 * q : 4 * q + 4, :].rearrange("a r n -> r a n"),
+            )
+        load_words(key_table[1], tab_words[1])
         for b in range(2):
             nc.sync.dma_start(
                 out=wg_raw[b][:], in_=wg[b * PASS : (b + 1) * PASS, :].rearrange("(p t) n -> p t n", t=PACK)
             )
         nc.sync.dma_start(out=w4_codes[:], in_=w4_words.bitcast(I32).rearrange("a p c -> p a c"))
 
-        for tile, scales, row in ((query_scale_table, tab2_scales, QUERY_ROW[0]), (key_scale_table, tab_scales, KEY_ROW[0])):
-            for q in range(4):
-                nc.gpsimd.dma_start(
-                    out=tile[32 * q + row : 32 * q + row + 8, :], in_=scales.bitcast(I32)[:, 4 * q : 4 * q + 4, :]
-                )
-        for q in range(4):
-            nc.sync.dma_start(
-                out=w4_plane[32 * q : 32 * q + 4, :, :],
-                in_=w4_scales.bitcast(I32)[:, 4 * q : 4 * q + 4, :].rearrange("a r n -> r a n"),
-            )
-
         nc.scalar.activation(out=log_decay[:], in_=decay[:], func=ACT.Ln, scale=0.5)
         warm = keep.tile([P, 1], F32, name="warm")
         nc.scalar.activation(out=warm[:], in_=log_decay[:, 0, 0:1], func=ACT.Exp)
 
         keys = {}
-        queries = {0: keep.tile([P, S2], U32, name="queries0", align_bytes=64)}
-        key_plane_listed = keep.tile([P, S], U8, name="key_plane_listed", tag="slot_c", align_bytes=64)
+        queries = [keep.tile([P, S2], U32, name="queries%d" % a, align_bytes=64) for a in range(2)]
+        key_plane_listed = keep.tile([P, S], U8, name="key_plane_listed", align_bytes=64)
         key_plane = keep.tile([P, S], U8, name="key_plane", align_bytes=64)
         query_plane = keep.tile([P, S2], U8, name="query_plane", align_bytes=64)
 
@@ -106,8 +108,9 @@ def tile_list_decayed_key_read_kernel(
                 key_table[a][:].bitcast(U32).indirect(list_half(key_list, b)),
             )
 
-        for h in range(2):
-            gather_queries(0, h)
+        for a in range(2):
+            for h in range(2):
+                gather_queries(a, h)
         for h in range(2):
             nc.vector.tensor_copy(
                 query_plane[:, half(h)], query_scale_table[:].bitcast(U8).indirect(list_half(query_list, h))
@@ -160,9 +163,6 @@ def tile_list_decayed_key_read_kernel(
         keys[1] = keep.tile([P, S], U32, name="keys1", tag="slot_b", align_bytes=64)
         for b in range(2):
             gather_keys(1, b)
-        queries[1] = keep.tile([P, S2], U32, name="queries1", tag="slot_c", align_bytes=64)
-        for h in range(2):
-            gather_queries(1, h)
 
         def exponentials(accs, b):
             rows = ring.tile([P, PACK, BANK], BF16, name="rows", align_bytes=64)
@@ -182,7 +182,7 @@ def tile_list_decayed_key_read_kernel(
         rows = {}
         for b in range(2):
             rows[0, b] = exponentials(scores, b)
-        wg_grouped = keep.tile([P, N, PACK], BF16, name="wg_grouped0", tag="query_table1", align_bytes=64)
+        wg_grouped = keep.tile([P, N, PACK], BF16, name="wg_grouped0", tag="key_table1", align_bytes=64)
         interleave(wg_grouped, wg_raw[0])
         grouped = pack_rows(rows[0, 0])
         quantize(wg_codes[:, 0, :], wg_plane[:, 0, :], wg_grouped)

@@ -32,16 +32,16 @@ def tile_list_decayed_key_read_kernel(
         lists = ctx.enter_context(tc.tile_pool(name="lists", bufs=1))
         keep = ctx.enter_context(tc.tile_pool(name="keep", bufs=1))
         ring = ctx.enter_context(tc.tile_pool(name="ring", bufs=4))
-        tail = ctx.enter_context(tc.tile_pool(name="tail", bufs=4))
+        tail = ctx.enter_context(tc.tile_pool(name="tail", bufs=8))
         psum = ctx.enter_context(tc.psum_pool(name="psum", bufs=1))
 
         key_list = lists.tile([P, S // 16], U16, name="key_list")
         query_list = lists.tile([P, S2 // 16], U16, name="query_list")
 
-        key_table = [keep.tile([P, T], I32, name="key_table%d" % a, tag="key_table%d" % a, align_bytes=64) for a in range(2)]
-        query_table = [keep.tile([P, T2], I32, name="query_table%d" % a, tag="query_table%d" % a, align_bytes=64) for a in range(2)]
-        key_scale_table = keep.tile([P, T // 4], I32, name="key_scale_table", tag="slot_b", align_bytes=64)
-        query_scale_table = keep.tile([P, T2 // 4], I32, name="query_scale_table", tag="slot_a", align_bytes=64)
+        key_table = [keep.tile([P, T], I32, name="key_table%d" % a, align_bytes=64) for a in range(2)]
+        query_table = [keep.tile([P, T2], I32, name="query_table%d" % a, align_bytes=64) for a in range(2)]
+        key_scale_table = keep.tile([P, T // 4], I32, name="key_scale_table", align_bytes=64)
+        query_scale_table = keep.tile([P, T2 // 4], I32, name="query_scale_table", align_bytes=64)
         w4_codes = keep.tile([P, 2, N // 2], I32, name="w4_codes", align_bytes=64)
         w4_plane = keep.tile([P, 2, N // 4], I32, name="w4_plane", align_bytes=64)
         wg_raw = [keep.tile([P, PACK, N], F32, name="wg_raw%d" % b, align_bytes=64) for b in range(2)]
@@ -52,40 +52,53 @@ def tile_list_decayed_key_read_kernel(
         nc.gpsimd.memset(key_scale_table[:], 0)
         nc.vector.memset(w4_plane[:], 0)
 
-        def load_words(tile, words):
-            nc.sync.dma_start(out=tile[:], in_=words.rearrange("p t i -> p (t i)").bitcast(I32))
+        def load_words(tile, words, cols):
+            nc.sync.dma_start(out=tile[:, cols], in_=words.rearrange("p t i -> p (t i)").bitcast(I32)[:, cols])
 
-        def load_scale_rows(queue, tile, scales, row):
-            for q in range(4):
-                queue.dma_start(
-                    out=tile[32 * q + row : 32 * q + row + 8, :], in_=scales.bitcast(I32)[:, 4 * q : 4 * q + 4, :]
+        def load_key_quarter(c):
+            load_words(key_table[0], tab_words[0], slice(c * T // 4, (c + 1) * T // 4))
+
+        def load_key_scale_rows(rows):
+            for a, r in rows:
+                nc.sync.dma_start(
+                    out=key_scale_table[KEY_ROW[a] + r : P : 32, :], in_=tab_scales.bitcast(I32)[a, r:16:4, :]
                 )
 
-        load_scale_rows(nc.gpsimd, key_scale_table, tab_scales, KEY_ROW[0])
+        key_rows = [(a, r) for r in range(4) for a in range(2)]
+        load_words(query_table[0], tab2_words[0], slice(0, T2))
         nc.sync.dma_start(query_list[:], offs2)
-        load_words(query_table[0], tab2_words[0])
-        load_words(query_table[1], tab2_words[1])
         nc.sync.dma_start(key_list[:], offs)
-        nc.sync.dma_start(out=decay[:], in_=dec.rearrange("(b p t) -> p b t", b=2, t=PACK))
-        load_scale_rows(nc.sync, query_scale_table, tab2_scales, QUERY_ROW[0])
-        load_words(key_table[0], tab_words[0])
+        load_key_quarter(0)
         for q in range(4):
+            row = 32 * q + QUERY_ROW[0]
             nc.sync.dma_start(
-                out=w4_plane[32 * q : 32 * q + 4, :, :],
-                in_=w4_scales.bitcast(I32)[:, 4 * q : 4 * q + 4, :].rearrange("a r n -> r a n"),
+                out=query_scale_table[row : row + 8, :], in_=tab2_scales.bitcast(I32)[:, 4 * q : 4 * q + 4, :]
             )
-        load_words(key_table[1], tab_words[1])
+        load_key_scale_rows(key_rows[0:3])
+        load_key_quarter(1)
+        load_key_scale_rows(key_rows[3:6])
+        load_key_quarter(2)
+        load_key_scale_rows(key_rows[6:8])
+        nc.sync.dma_start(out=decay[:], in_=dec.rearrange("(b p t) -> p b t", b=2, t=PACK))
+        load_key_quarter(3)
+        load_words(query_table[1], tab2_words[1], slice(0, T2))
+        load_words(key_table[1], tab_words[1], slice(0, T))
         for b in range(2):
             nc.sync.dma_start(
                 out=wg_raw[b][:], in_=wg[b * PASS : (b + 1) * PASS, :].rearrange("(p t) n -> p t n", t=PACK)
             )
         nc.sync.dma_start(out=w4_codes[:], in_=w4_words.bitcast(I32).rearrange("a p c -> p a c"))
+        for q in range(4):
+            nc.sync.dma_start(
+                out=w4_plane[32 * q : 32 * q + 4, :, :],
+                in_=w4_scales.bitcast(I32)[:, 4 * q : 4 * q + 4, :].rearrange("a r n -> r a n"),
+            )
 
         nc.scalar.activation(out=log_decay[:], in_=decay[:], func=ACT.Ln, scale=0.5)
         warm = keep.tile([P, 1], F32, name="warm")
         nc.scalar.activation(out=warm[:], in_=log_decay[:, 0, 0:1], func=ACT.Exp)
 
-        keys = {}
+        keys = [keep.tile([P, S], U32, name="keys%d" % a, align_bytes=64) for a in range(2)]
         queries = [keep.tile([P, S2], U32, name="queries%d" % a, align_bytes=64) for a in range(2)]
         key_plane_listed = keep.tile([P, S], U8, name="key_plane_listed", align_bytes=64)
         key_plane = keep.tile([P, S], U8, name="key_plane", align_bytes=64)
@@ -97,10 +110,8 @@ def tile_list_decayed_key_read_kernel(
         def list_half(tile, h):
             return tile[:, h * (BANK // 16) : (h + 1) * (BANK // 16)]
 
-        def gather_queries(a, h):
-            nc.vector.tensor_copy(
-                queries[a][:, half(h)], query_table[a][:].bitcast(U32).indirect(list_half(query_list, h))
-            )
+        def gather_queries(a):
+            nc.vector.tensor_copy(queries[a][:], query_table[a][:].bitcast(U32).indirect(query_list[:]))
 
         def gather_keys(a, b):
             nc.vector.tensor_copy(
@@ -108,24 +119,15 @@ def tile_list_decayed_key_read_kernel(
                 key_table[a][:].bitcast(U32).indirect(list_half(key_list, b)),
             )
 
-        for a in range(2):
-            for h in range(2):
-                gather_queries(a, h)
-        for h in range(2):
-            nc.vector.tensor_copy(
-                query_plane[:, half(h)], query_scale_table[:].bitcast(U8).indirect(list_half(query_list, h))
-            )
-        keys[0] = keep.tile([P, S], U32, name="keys0", tag="slot_a", align_bytes=64)
-        for b in range(2):
-            gather_keys(0, b)
-        for b in range(2):
-            nc.vector.tensor_copy(
-                key_plane_listed[:, half(b)], key_scale_table[:].bitcast(U8).indirect(list_half(key_list, b))
-            )
+        gather_queries(0)
+        nc.vector.tensor_copy(query_plane[:], query_scale_table[:].bitcast(U8).indirect(query_list[:]))
+        nc.vector.tensor_copy(key_plane_listed[:], key_scale_table[:].bitcast(U8).indirect(key_list[:]))
         nc.vector.tensor_copy(
             key_plane[:].rearrange("p (b t m) -> p b t m", b=2, t=PACK),
             key_plane_listed[:].rearrange("p (b m t) -> p b t m", b=2, t=PACK),
         )
+        for b in range(2):
+            gather_keys(0, b)
 
         def bank(n):
             return psum.tile([P, BANK], F32, name="bank%d" % n)
@@ -160,7 +162,7 @@ def tile_list_decayed_key_read_kernel(
         scores = [bank(n) for n in range(8)]
         for n in range(8):
             score_pass(scores[n], 0, n, 0)
-        keys[1] = keep.tile([P, S], U32, name="keys1", tag="slot_b", align_bytes=64)
+        gather_queries(1)
         for b in range(2):
             gather_keys(1, b)
 
@@ -182,8 +184,7 @@ def tile_list_decayed_key_read_kernel(
         rows = {}
         for b in range(2):
             rows[0, b] = exponentials(scores, b)
-        wg_grouped = keep.tile([P, N, PACK], BF16, name="wg_grouped0", tag="key_table1", align_bytes=64)
-        interleave(wg_grouped, wg_raw[0])
+        wg_grouped = pack_rows(wg_raw[0])
         grouped = pack_rows(rows[0, 0])
         quantize(wg_codes[:, 0, :], wg_plane[:, 0, :], wg_grouped)
         quantize(p_codes[0][:, 0, :], p_plane[0][:, 0, :], grouped)
@@ -220,14 +221,18 @@ def tile_list_decayed_key_read_kernel(
                 stop=(b == 1),
             )
 
-        def finish(gate, value, n, h):
-            damp = tail.tile([P, BANK], F32, name="damp")
-            nc.scalar.activation(out=damp[:], in_=gate[:], func=ACT.Tanh)
-            result = tail.tile([P, BANK], F32, name="result")
-            nc.vector.scalar_tensor_tensor(
-                out=result[:], in0=damp[:], scalar=1.0, in1=value[:], op0=ALU.add, op1=ALU.mult
-            )
-            nc.sync.dma_start(out=out[n * P : (n + 1) * P, half(h)], in_=result[:])
+        def finish(gate, value, n, h, pieces):
+            width = BANK // pieces
+            for c in range(0, BANK, width):
+                damp = tail.tile([P, width], F32, name="damp")
+                nc.scalar.activation(out=damp[:], in_=gate[:, c : c + width], func=ACT.Tanh)
+                result = tail.tile([P, width], F32, name="result")
+                nc.vector.scalar_tensor_tensor(
+                    out=result[:], in0=damp[:], scalar=1.0, in1=value[:, c : c + width], op0=ALU.add, op1=ALU.mult
+                )
+                nc.sync.dma_start(
+                    out=out[n * P : (n + 1) * P, h * BANK + c : h * BANK + c + width], in_=result[:]
+                )
 
         reads = [bank(n) for n in range(8)]
         for n in range(4):
@@ -237,10 +242,10 @@ def tile_list_decayed_key_read_kernel(
         for b in range(2):
             quantize(p_codes[1][:, b, :], p_plane[1][:, b, :], both[b])
         for n in range(4):
-            finish(reads[2 * n], reads[2 * n + 1], n, 0)
+            finish(reads[2 * n], reads[2 * n + 1], n, 0, 1)
         reads = [bank(n) for n in range(8)]
         for n in range(4):
             for b in range(2):
                 read_pass(reads[2 * n], reads[2 * n + 1], n, 1, b)
         for n in range(4):
-            finish(reads[2 * n], reads[2 * n + 1], n, 1)
+            finish(reads[2 * n], reads[2 * n + 1], n, 1, 2 if n == 3 else 1)

@@ -20,8 +20,8 @@ P = 128
 PACK = 4
 PASS = P * PACK
 BANK = 512
-KEY_ROW = (0, 4)
-QUERY_ROW = (8, 12)
+PLANE_ROW = (0, 4)
+DENSE = 96
 
 
 def tile_list_decayed_key_read_kernel(
@@ -48,51 +48,28 @@ def tile_list_decayed_key_read_kernel(
         decay = keep.tile([P, 2, PACK], F32, name="decay")
         log_decay = keep.tile([P, 2, PACK], F32, name="log_decay")
 
-        nc.vector.memset(query_scale_table[:], 0)
-        nc.gpsimd.memset(key_scale_table[:], 0)
-        nc.vector.memset(w4_plane[:], 0)
+        planes = [keep.tile([P, (S + S2) // 4], I32, name="planes%d" % a, align_bytes=64) for a in range(2)]
+        nc.vector.memset(query_scale_table[0:DENSE, :], 0)
+        nc.vector.memset(key_scale_table[0:DENSE, :], 0)
+        nc.vector.memset(planes[0][:], 0)
+        nc.gpsimd.memset(planes[1][:], 0)
+        nc.gpsimd.memset(w4_plane[:], 0)
 
         def load_words(tile, words, cols):
             nc.sync.dma_start(out=tile[:, cols], in_=words.rearrange("p t i -> p (t i)").bitcast(I32)[:, cols])
 
-        def load_key_quarter(c):
-            load_words(key_table[0], tab_words[0], slice(c * T // 4, (c + 1) * T // 4))
+        def load_key_half(a, c):
+            load_words(key_table[a], tab_words[a], slice(c * T // 2, (c + 1) * T // 2))
 
-        def load_key_scale_rows(rows):
-            for a, r in rows:
-                nc.sync.dma_start(
-                    out=key_scale_table[KEY_ROW[a] + r : P : 32, :], in_=tab_scales.bitcast(I32)[a, r:16:4, :]
-                )
-
-        key_rows = [(a, r) for r in range(4) for a in range(2)]
-        load_words(query_table[0], tab2_words[0], slice(0, T2))
+        nc.sync.dma_start(out=query_scale_table[DENSE:P, :], in_=tab2_scales.bitcast(I32).rearrange("a q t -> (a q) t"))
         nc.sync.dma_start(query_list[:], offs2)
+        nc.sync.dma_start(out=key_scale_table[DENSE:P, :], in_=tab_scales.bitcast(I32).rearrange("a q t -> (a q) t"))
         nc.sync.dma_start(key_list[:], offs)
-        load_key_quarter(0)
-        for q in range(4):
-            row = 32 * q + QUERY_ROW[0]
-            nc.sync.dma_start(
-                out=query_scale_table[row : row + 8, :], in_=tab2_scales.bitcast(I32)[:, 4 * q : 4 * q + 4, :]
-            )
-        load_key_scale_rows(key_rows[0:3])
-        load_key_quarter(1)
-        load_key_scale_rows(key_rows[3:6])
-        load_key_quarter(2)
-        load_key_scale_rows(key_rows[6:8])
-        nc.sync.dma_start(out=decay[:], in_=dec.rearrange("(b p t) -> p b t", b=2, t=PACK))
-        load_key_quarter(3)
+        load_words(query_table[0], tab2_words[0], slice(0, T2))
         load_words(query_table[1], tab2_words[1], slice(0, T2))
-        load_words(key_table[1], tab_words[1], slice(0, T))
-        for b in range(2):
-            nc.sync.dma_start(
-                out=wg_raw[b][:], in_=wg[b * PASS : (b + 1) * PASS, :].rearrange("(p t) n -> p t n", t=PACK)
-            )
-        nc.sync.dma_start(out=w4_codes[:], in_=w4_words.bitcast(I32).rearrange("a p c -> p a c"))
-        for q in range(4):
-            nc.sync.dma_start(
-                out=w4_plane[32 * q : 32 * q + 4, :, :],
-                in_=w4_scales.bitcast(I32)[:, 4 * q : 4 * q + 4, :].rearrange("a r n -> r a n"),
-            )
+        load_key_half(0, 0)
+        load_key_half(0, 1)
+        nc.sync.dma_start(out=decay[:], in_=dec.rearrange("(b p t) -> p b t", b=2, t=PACK))
 
         nc.scalar.activation(out=log_decay[:], in_=decay[:], func=ACT.Ln, scale=0.5)
         warm = keep.tile([P, 1], F32, name="warm")
@@ -101,8 +78,8 @@ def tile_list_decayed_key_read_kernel(
         keys = [keep.tile([P, S], U32, name="keys%d" % a, align_bytes=64) for a in range(2)]
         queries = [keep.tile([P, S2], U32, name="queries%d" % a, align_bytes=64) for a in range(2)]
         key_plane_listed = keep.tile([P, S], U8, name="key_plane_listed", align_bytes=64)
-        key_plane = keep.tile([P, S], U8, name="key_plane", align_bytes=64)
-        query_plane = keep.tile([P, S2], U8, name="query_plane", align_bytes=64)
+        query_plane_listed = keep.tile([P, S2], U8, name="query_plane_listed", align_bytes=64)
+        dense_planes = keep.tile([P, S + S2], U8, name="dense_planes", align_bytes=64)
 
         def half(h):
             return slice(h * BANK, (h + 1) * BANK)
@@ -119,13 +96,39 @@ def tile_list_decayed_key_read_kernel(
                 key_table[a][:].bitcast(U32).indirect(list_half(key_list, b)),
             )
 
-        gather_queries(0)
-        nc.vector.tensor_copy(query_plane[:], query_scale_table[:].bitcast(U8).indirect(query_list[:]))
+        nc.vector.tensor_copy(query_plane_listed[:], query_scale_table[:].bitcast(U8).indirect(query_list[:]))
         nc.vector.tensor_copy(key_plane_listed[:], key_scale_table[:].bitcast(U8).indirect(key_list[:]))
+        nc.vector.tensor_copy(dense_planes[:, S:].bitcast(I32), query_plane_listed[:].bitcast(I32))
         nc.vector.tensor_copy(
-            key_plane[:].rearrange("p (b t m) -> p b t m", b=2, t=PACK),
+            dense_planes[:, :S].rearrange("p (b t m) -> p b t m", b=2, t=PACK),
             key_plane_listed[:].rearrange("p (b m t) -> p b t m", b=2, t=PACK),
         )
+
+        def place_scale_rows(a, rows):
+            for r in rows:
+                first = DENSE + 16 * a + r
+                nc.sync.dma_start(
+                    out=planes[a][PLANE_ROW[a] + r : P : 32, :],
+                    in_=dense_planes[first : first + 13 : 4, :].bitcast(I32),
+                )
+
+        place_scale_rows(0, range(4))
+        load_key_half(1, 0)
+        place_scale_rows(1, range(4))
+        load_key_half(1, 1)
+        for b in range(2):
+            nc.sync.dma_start(
+                out=wg_raw[b][:], in_=wg[b * PASS : (b + 1) * PASS, :].rearrange("(p t) n -> p t n", t=PACK)
+            )
+        nc.sync.dma_start(out=w4_codes[:], in_=w4_words.bitcast(I32).rearrange("a p c -> p a c"))
+        for q in range(4):
+            nc.sync.dma_start(
+                out=w4_plane[32 * q : 32 * q + 4, :, :],
+                in_=w4_scales.bitcast(I32)[:, 4 * q : 4 * q + 4, :].rearrange("a r n -> r a n"),
+            )
+
+        for a in range(2):
+            gather_queries(a)
         for b in range(2):
             gather_keys(0, b)
 
@@ -137,9 +140,9 @@ def tile_list_decayed_key_read_kernel(
             nc.tensor.matmul_mx(
                 out=acc[:],
                 lhsT=keys[a][:, cols].bitcast(FP8X4),
-                lhsT_scale=key_plane[KEY_ROW[a] : P, cols],
+                lhsT_scale=planes[a][PLANE_ROW[a] : P, :].bitcast(U8)[:, cols],
                 rhs=queries[a][:, half(h)].bitcast(FP8X4),
-                rhs_scale=query_plane[QUERY_ROW[a] : P, half(h)],
+                rhs_scale=planes[a][PLANE_ROW[a] : P, :].bitcast(U8)[:, S + h * BANK : S + (h + 1) * BANK],
                 start=(a == 0),
                 stop=(a == 1),
             )
@@ -162,7 +165,6 @@ def tile_list_decayed_key_read_kernel(
         scores = [bank(n) for n in range(8)]
         for n in range(8):
             score_pass(scores[n], 0, n, 0)
-        gather_queries(1)
         for b in range(2):
             gather_keys(1, b)
 

@@ -112,10 +112,10 @@ def tile_list_decayed_key_read_kernel(
                     in_=dense_planes[first : first + 13 : 4, :].bitcast(I32),
                 )
 
-        place_scale_rows(0, range(4))
         load_key_half(1, 0)
-        place_scale_rows(1, range(4))
+        place_scale_rows(0, range(4))
         load_key_half(1, 1)
+        place_scale_rows(1, range(4))
         for b in range(2):
             nc.sync.dma_start(
                 out=wg_raw[b][:], in_=wg[b * PASS : (b + 1) * PASS, :].rearrange("(p t) n -> p t n", t=PACK)
@@ -186,9 +186,9 @@ def tile_list_decayed_key_read_kernel(
         rows = {}
         for b in range(2):
             rows[0, b] = exponentials(scores, b)
-        wg_grouped = pack_rows(wg_raw[0])
+        quantize(wg_codes[:, 0, :], wg_plane[:, 0, :], pack_rows(wg_raw[0]))
         grouped = pack_rows(rows[0, 0])
-        quantize(wg_codes[:, 0, :], wg_plane[:, 0, :], wg_grouped)
+        wg_grouped = pack_rows(wg_raw[1])
         quantize(p_codes[0][:, 0, :], p_plane[0][:, 0, :], grouped)
 
         scores = [bank(n) for n in range(8)]
@@ -197,7 +197,6 @@ def tile_list_decayed_key_read_kernel(
                 score_pass(scores[n], a, n, 1)
         for b in range(2):
             rows[1, b] = exponentials(scores, b)
-        wg_grouped = pack_rows(wg_raw[1])
         grouped = pack_rows(rows[0, 1])
         quantize(wg_codes[:, 1, :], wg_plane[:, 1, :], wg_grouped)
         quantize(p_codes[0][:, 1, :], p_plane[0][:, 1, :], grouped)
@@ -240,13 +239,18 @@ def tile_list_decayed_key_read_kernel(
         for n in range(4):
             for b in range(2):
                 read_pass(reads[2 * n], reads[2 * n + 1], n, 0, b)
-        both = [pack_rows(rows[1, b]) for b in range(2)]
-        for b in range(2):
-            quantize(p_codes[1][:, b, :], p_plane[1][:, b, :], both[b])
-        for n in range(4):
+        quantize(p_codes[1][:, 0, :], p_plane[1][:, 0, :], pack_rows(rows[1, 0]))
+        grouped = pack_rows(rows[1, 1])
+        finish(reads[0], reads[1], 0, 0, 1)
+        quantize(p_codes[1][:, 1, :], p_plane[1][:, 1, :], grouped)
+        for n in range(1, 4):
             finish(reads[2 * n], reads[2 * n + 1], n, 0, 1)
         reads = [bank(n) for n in range(8)]
-        for n in range(4):
+        for n in range(2):
+            read_pass(reads[2 * n], reads[2 * n + 1], n, 1, 0)
+        for n in range(2):
+            read_pass(reads[2 * n], reads[2 * n + 1], n, 1, 1)
+        for n in range(2, 4):
             for b in range(2):
                 read_pass(reads[2 * n], reads[2 * n + 1], n, 1, b)
         for n in range(4):

@@ -61,12 +61,14 @@ def tile_list_decayed_key_read_kernel(
         def load_key_half(a, c):
             load_words(key_table[a], tab_words[a], slice(c * T // 2, (c + 1) * T // 2))
 
-        nc.sync.dma_start(out=query_scale_table[DENSE:P, :], in_=tab2_scales.bitcast(I32).rearrange("a q t -> (a q) t"))
+        def load_scale_rows(tile, scales):
+            nc.sync.dma_start(out=tile[DENSE:P, :], in_=scales.bitcast(I32).rearrange("a q t -> (a q) t"))
+
+        load_scale_rows(query_scale_table, tab2_scales)
         nc.sync.dma_start(query_list[:], offs2)
-        nc.sync.dma_start(out=key_scale_table[DENSE:P, :], in_=tab_scales.bitcast(I32).rearrange("a q t -> (a q) t"))
+        load_scale_rows(key_scale_table, tab_scales)
         nc.sync.dma_start(key_list[:], offs)
         load_words(query_table[0], tab2_words[0], slice(0, T2))
-        load_words(query_table[1], tab2_words[1], slice(0, T2))
         load_key_half(0, 0)
         load_key_half(0, 1)
         nc.sync.dma_start(out=decay[:], in_=dec.rearrange("(b p t) -> p b t", b=2, t=PACK))
@@ -87,8 +89,10 @@ def tile_list_decayed_key_read_kernel(
         def list_half(tile, h):
             return tile[:, h * (BANK // 16) : (h + 1) * (BANK // 16)]
 
-        def gather_queries(a):
-            nc.vector.tensor_copy(queries[a][:], query_table[a][:].bitcast(U32).indirect(query_list[:]))
+        def gather_queries(a, first, last):
+            nc.vector.tensor_copy(
+                queries[a][:, first:last], query_table[a][:].bitcast(U32).indirect(query_list[:, first // 16 : last // 16])
+            )
 
         def gather_keys(a, b):
             nc.vector.tensor_copy(
@@ -104,8 +108,8 @@ def tile_list_decayed_key_read_kernel(
             key_plane_listed[:].rearrange("p (b m t) -> p b t m", b=2, t=PACK),
         )
 
-        def place_scale_rows(a, rows):
-            for r in rows:
+        def place_scale_rows(a):
+            for r in range(4):
                 first = DENSE + 16 * a + r
                 nc.sync.dma_start(
                     out=planes[a][PLANE_ROW[a] + r : P : 32, :],
@@ -113,9 +117,10 @@ def tile_list_decayed_key_read_kernel(
                 )
 
         load_key_half(1, 0)
-        place_scale_rows(0, range(4))
+        place_scale_rows(0)
         load_key_half(1, 1)
-        place_scale_rows(1, range(4))
+        load_words(query_table[1], tab2_words[1], slice(0, T2))
+        place_scale_rows(1)
         for b in range(2):
             nc.sync.dma_start(
                 out=wg_raw[b][:], in_=wg[b * PASS : (b + 1) * PASS, :].rearrange("(p t) n -> p t n", t=PACK)
@@ -127,29 +132,30 @@ def tile_list_decayed_key_read_kernel(
                 in_=w4_scales.bitcast(I32)[:, 4 * q : 4 * q + 4, :].rearrange("a r n -> r a n"),
             )
 
+        gather_queries(0, 0, S2)
         for a in range(2):
-            gather_queries(a)
-        for b in range(2):
-            gather_keys(0, b)
+            for b in range(2):
+                gather_keys(a, b)
 
         def bank(n):
             return psum.tile([P, BANK], F32, name="bank%d" % n)
 
-        def score_pass(acc, a, tile_index, h):
+        def score_pass(acc, a, tile_index, h, first=0, last=BANK):
             cols = slice(tile_index * P, (tile_index + 1) * P)
             nc.tensor.matmul_mx(
-                out=acc[:],
+                out=acc[:, first:last],
                 lhsT=keys[a][:, cols].bitcast(FP8X4),
                 lhsT_scale=planes[a][PLANE_ROW[a] : P, :].bitcast(U8)[:, cols],
-                rhs=queries[a][:, half(h)].bitcast(FP8X4),
-                rhs_scale=planes[a][PLANE_ROW[a] : P, :].bitcast(U8)[:, S + h * BANK : S + (h + 1) * BANK],
+                rhs=queries[a][:, h * BANK + first : h * BANK + last].bitcast(FP8X4),
+                rhs_scale=planes[a][PLANE_ROW[a] : P, :].bitcast(U8)[:, S + h * BANK + first : S + h * BANK + last],
                 start=(a == 0),
-                stop=(a == 1),
+                stop=(a == 1 and last == BANK),
             )
 
-        def interleave(dst, src):
-            nc.vector.tensor_copy(
-                out=dst[:].rearrange("p (c i) t -> p c t i", i=4), in_=src[:].rearrange("p t (c i) -> p c t i", i=4)
+        def interleave(copy, dst, src, first, last):
+            copy(
+                out=dst[:, first:last, :].rearrange("p (c i) t -> p c t i", i=4),
+                in_=src[:, :, first:last].rearrange("p t (c i) -> p c t i", i=4),
             )
 
         def quantize(codes, plane, grouped):
@@ -165,8 +171,8 @@ def tile_list_decayed_key_read_kernel(
         scores = [bank(n) for n in range(8)]
         for n in range(8):
             score_pass(scores[n], 0, n, 0)
-        for b in range(2):
-            gather_keys(1, b)
+        for first, last in ((0, BANK // 2), (BANK // 2, BANK), (BANK, S2)):
+            gather_queries(1, first, last)
 
         def exponentials(accs, b):
             rows = ring.tile([P, PACK, BANK], BF16, name="rows", align_bytes=64)
@@ -176,19 +182,24 @@ def tile_list_decayed_key_read_kernel(
                 )
             return rows
 
-        def pack_rows(rows):
-            grouped = ring.tile([P, BANK, PACK], BF16, name="grouped", align_bytes=64)
-            interleave(grouped, rows)
+        def pack_rows(rows, slot, scalar_share=0):
+            grouped = keep.tile([P, BANK, PACK], BF16, name="grouped%d" % slot, align_bytes=64)
+            if scalar_share:
+                interleave(nc.scalar.copy, grouped, rows, 0, scalar_share)
+            interleave(nc.vector.tensor_copy, grouped, rows, scalar_share, BANK)
             return grouped
 
-        for n in range(8):
+        for first in (0, BANK // 2):
+            for n in range(4):
+                score_pass(scores[n], 1, n, 0, first, first + BANK // 2)
+        for n in range(4, 8):
             score_pass(scores[n], 1, n, 0)
         rows = {}
         for b in range(2):
             rows[0, b] = exponentials(scores, b)
-        quantize(wg_codes[:, 0, :], wg_plane[:, 0, :], pack_rows(wg_raw[0]))
-        grouped = pack_rows(rows[0, 0])
-        wg_grouped = pack_rows(wg_raw[1])
+        wg_grouped = pack_rows(wg_raw[0], 0)
+        grouped = pack_rows(rows[0, 0], 1)
+        quantize(wg_codes[:, 0, :], wg_plane[:, 0, :], wg_grouped)
         quantize(p_codes[0][:, 0, :], p_plane[0][:, 0, :], grouped)
 
         scores = [bank(n) for n in range(8)]
@@ -197,11 +208,16 @@ def tile_list_decayed_key_read_kernel(
                 score_pass(scores[n], a, n, 1)
         for b in range(2):
             rows[1, b] = exponentials(scores, b)
-        grouped = pack_rows(rows[0, 1])
-        quantize(wg_codes[:, 1, :], wg_plane[:, 1, :], wg_grouped)
+        grouped = pack_rows(rows[0, 1], 0)
+        wg_grouped = pack_rows(wg_raw[1], 1)
         quantize(p_codes[0][:, 1, :], p_plane[0][:, 1, :], grouped)
+        quantize(wg_codes[:, 1, :], wg_plane[:, 1, :], wg_grouped)
+        for b in range(2):
+            rows[1, b] = pack_rows(rows[1, b], b, b * BANK // 2)
+        for b in range(2):
+            quantize(p_codes[1][:, b, :], p_plane[1][:, b, :], rows[1, b])
 
-        def read_pass(gate, value, n, h, b):
+        def gate_pass(gate, n, h, b):
             cols = slice(n * P, (n + 1) * P)
             nc.tensor.matmul_mx(
                 out=gate[:],
@@ -212,6 +228,9 @@ def tile_list_decayed_key_read_kernel(
                 start=(b == 0),
                 stop=(b == 1),
             )
+
+        def value_pass(value, n, h, b):
+            cols = slice(n * P, (n + 1) * P)
             nc.tensor.matmul_mx(
                 out=value[:],
                 lhsT=w4_codes[:, b, n * (P // 2) : (n + 1) * (P // 2)].bitcast(FP4X4),
@@ -236,22 +255,26 @@ def tile_list_decayed_key_read_kernel(
                 )
 
         reads = [bank(n) for n in range(8)]
-        for n in range(4):
-            for b in range(2):
-                read_pass(reads[2 * n], reads[2 * n + 1], n, 0, b)
-        quantize(p_codes[1][:, 0, :], p_plane[1][:, 0, :], pack_rows(rows[1, 0]))
-        grouped = pack_rows(rows[1, 1])
-        finish(reads[0], reads[1], 0, 0, 1)
-        quantize(p_codes[1][:, 1, :], p_plane[1][:, 1, :], grouped)
-        for n in range(1, 4):
-            finish(reads[2 * n], reads[2 * n + 1], n, 0, 1)
-        reads = [bank(n) for n in range(8)]
         for n in range(2):
-            read_pass(reads[2 * n], reads[2 * n + 1], n, 1, 0)
+            gate_pass(reads[2 * n], n, 0, 0)
+            value_pass(reads[2 * n + 1], n, 0, 0)
         for n in range(2):
-            read_pass(reads[2 * n], reads[2 * n + 1], n, 1, 1)
+            value_pass(reads[2 * n + 1], n, 0, 1)
+        for n in range(2):
+            gate_pass(reads[2 * n], n, 0, 1)
         for n in range(2, 4):
             for b in range(2):
-                read_pass(reads[2 * n], reads[2 * n + 1], n, 1, b)
+                gate_pass(reads[2 * n], n, 0, b)
+            for b in range(2):
+                value_pass(reads[2 * n + 1], n, 0, b)
+        for n in range(4):
+            finish(reads[2 * n], reads[2 * n + 1], n, 0, 1)
+        reads = [bank(n) for n in range(8)]
+        for b in range(2):
+            for n in range(4):
+                gate_pass(reads[2 * n], n, 1, b)
+        for n in range(4):
+            for b in range(2):
+                value_pass(reads[2 * n + 1], n, 1, b)
         for n in range(4):
             finish(reads[2 * n], reads[2 * n + 1], n, 1, 2 if n == 3 else 1)

@@ -71,7 +71,7 @@ def tile_list_decayed_key_read_kernel(
         load_words(query_table[0], tab2_words[0], slice(0, T2))
         load_key_half(0, 0)
         load_key_half(0, 1)
-        nc.sync.dma_start(out=decay[:], in_=dec.rearrange("(b p t) -> p b t", b=2, t=PACK))
+        nc.scalar.dma_start(out=decay[:], in_=dec.rearrange("(b p t) -> p b t", b=2, t=PACK))
 
         nc.scalar.activation(out=log_decay[:], in_=decay[:], func=ACT.Ln, scale=0.5)
         warm = keep.tile([P, 1], F32, name="warm")
@@ -121,11 +121,14 @@ def tile_list_decayed_key_read_kernel(
         load_key_half(1, 1)
         load_words(query_table[1], tab2_words[1], slice(0, T2))
         place_scale_rows(1)
-        for b in range(2):
+        def load_wg(b):
             nc.sync.dma_start(
                 out=wg_raw[b][:], in_=wg[b * PASS : (b + 1) * PASS, :].rearrange("(p t) n -> p t n", t=PACK)
             )
+
+        load_wg(0)
         nc.sync.dma_start(out=w4_codes[:], in_=w4_words.bitcast(I32).rearrange("a p c -> p a c"))
+        load_wg(1)
         for q in range(4):
             nc.sync.dma_start(
                 out=w4_plane[32 * q : 32 * q + 4, :, :],
@@ -152,16 +155,11 @@ def tile_list_decayed_key_read_kernel(
                 stop=(a == 1 and last == BANK),
             )
 
-        def interleave(copy, dst, src, first, last):
-            copy(
-                out=dst[:, first:last, :].rearrange("p (c i) t -> p c t i", i=4),
-                in_=src[:, :, first:last].rearrange("p t (c i) -> p c t i", i=4),
-            )
+        def interleave(copy, dst, src):
+            copy(out=dst.rearrange("p (c i) t -> p c t i", i=4), in_=src.rearrange("p t (c i) -> p c t i", i=4))
 
         def quantize(codes, plane, grouped):
-            nc.vector.quantize_mx(
-                out=codes.bitcast(FP8X4), scales=plane, in_=grouped[:].rearrange("p n t -> p (n t)")
-            )
+            nc.vector.quantize_mx(out=codes.bitcast(FP8X4), scales=plane, in_=grouped[:].rearrange("p n t -> p (n t)"))
 
         wg_codes = keep.tile([P, 2, N], U32, name="wg_codes", align_bytes=64)
         wg_plane = keep.tile([P, 2, N], U8, name="wg_plane", align_bytes=64)
@@ -182,11 +180,9 @@ def tile_list_decayed_key_read_kernel(
                 )
             return rows
 
-        def pack_rows(rows, slot, scalar_share=0):
-            grouped = keep.tile([P, BANK, PACK], BF16, name="grouped%d" % slot, align_bytes=64)
-            if scalar_share:
-                interleave(nc.scalar.copy, grouped, rows, 0, scalar_share)
-            interleave(nc.vector.tensor_copy, grouped, rows, scalar_share, BANK)
+        def pack_rows(rows, slot, copy=nc.vector.tensor_copy, first=0, last=BANK):
+            grouped = keep.tile([P, last - first, PACK], BF16, name=slot, align_bytes=64)
+            interleave(copy, grouped[:], rows[:, :, first:last])
             return grouped
 
         for first in (0, BANK // 2):
@@ -197,8 +193,8 @@ def tile_list_decayed_key_read_kernel(
         rows = {}
         for b in range(2):
             rows[0, b] = exponentials(scores, b)
-        wg_grouped = pack_rows(wg_raw[0], 0)
-        grouped = pack_rows(rows[0, 0], 1)
+        wg_grouped = pack_rows(wg_raw[0], "grouped0")
+        grouped = pack_rows(rows[0, 0], "wg_raw0")
         quantize(wg_codes[:, 0, :], wg_plane[:, 0, :], wg_grouped)
         quantize(p_codes[0][:, 0, :], p_plane[0][:, 0, :], grouped)
 
@@ -208,14 +204,16 @@ def tile_list_decayed_key_read_kernel(
                 score_pass(scores[n], a, n, 1)
         for b in range(2):
             rows[1, b] = exponentials(scores, b)
-        grouped = pack_rows(rows[0, 1], 0)
-        wg_grouped = pack_rows(wg_raw[1], 1)
+        grouped = pack_rows(rows[0, 1], "grouped0")
+        wg_grouped = pack_rows(wg_raw[1], "wg_raw0")
         quantize(p_codes[0][:, 1, :], p_plane[0][:, 1, :], grouped)
         quantize(wg_codes[:, 1, :], wg_plane[:, 1, :], wg_grouped)
-        for b in range(2):
-            rows[1, b] = pack_rows(rows[1, b], b, b * BANK // 2)
-        for b in range(2):
-            quantize(p_codes[1][:, b, :], p_plane[1][:, b, :], rows[1, b])
+        grouped = pack_rows(rows[1, 0], "grouped0")
+        left = pack_rows(rows[1, 1], "grouped1", nc.scalar.copy, 0, 256)
+        right = pack_rows(rows[1, 1], "wg_raw0", nc.vector.tensor_copy, 256, BANK)
+        quantize(p_codes[1][:, 0, :], p_plane[1][:, 0, :], grouped)
+        quantize(p_codes[1][:, 1, :256], p_plane[1][:, 1, :256], left)
+        quantize(p_codes[1][:, 1, 256:], p_plane[1][:, 1, 256:], right)
 
         def gate_pass(gate, n, h, b):
             cols = slice(n * P, (n + 1) * P)
@@ -255,25 +253,16 @@ def tile_list_decayed_key_read_kernel(
                 )
 
         reads = [bank(n) for n in range(8)]
-        for n in range(2):
-            gate_pass(reads[2 * n], n, 0, 0)
-            value_pass(reads[2 * n + 1], n, 0, 0)
-        for n in range(2):
-            value_pass(reads[2 * n + 1], n, 0, 1)
-        for n in range(2):
-            gate_pass(reads[2 * n], n, 0, 1)
-        for n in range(2, 4):
+        for n in range(4):
             for b in range(2):
                 gate_pass(reads[2 * n], n, 0, b)
-            for b in range(2):
                 value_pass(reads[2 * n + 1], n, 0, b)
         for n in range(4):
             finish(reads[2 * n], reads[2 * n + 1], n, 0, 1)
         reads = [bank(n) for n in range(8)]
-        for b in range(2):
-            for n in range(4):
-                gate_pass(reads[2 * n], n, 1, b)
         for n in range(4):
+            for b in range(2):
+                gate_pass(reads[2 * n], n, 1, b)
             for b in range(2):
                 value_pass(reads[2 * n + 1], n, 1, b)
         for n in range(4):

@@ -52,8 +52,8 @@ def tile_list_decayed_key_read_kernel(
         nc.vector.memset(query_scale_table[0:DENSE, :], 0)
         nc.vector.memset(key_scale_table[0:DENSE, :], 0)
         nc.vector.memset(planes[0][:], 0)
-        nc.gpsimd.memset(planes[1][:], 0)
-        nc.gpsimd.memset(w4_plane[:], 0)
+        nc.vector.memset(planes[1][:], 0)
+        nc.vector.memset(w4_plane[:], 0)
 
         def load_words(tile, words, cols):
             nc.sync.dma_start(out=tile[:, cols], in_=words.rearrange("p t i -> p (t i)").bitcast(I32)[:, cols])
@@ -68,9 +68,9 @@ def tile_list_decayed_key_read_kernel(
         nc.sync.dma_start(query_list[:], offs2)
         load_scale_rows(key_scale_table, tab_scales)
         nc.sync.dma_start(key_list[:], offs)
-        load_words(query_table[0], tab2_words[0], slice(0, T2))
         load_key_half(0, 0)
         load_key_half(0, 1)
+        load_words(query_table[0], tab2_words[0], slice(0, T2))
         nc.scalar.dma_start(out=decay[:], in_=dec.rearrange("(b p t) -> p b t", b=2, t=PACK))
 
         nc.scalar.activation(out=log_decay[:], in_=decay[:], func=ACT.Ln, scale=0.5)
@@ -135,10 +135,11 @@ def tile_list_decayed_key_read_kernel(
                 in_=w4_scales.bitcast(I32)[:, 4 * q : 4 * q + 4, :].rearrange("a r n -> r a n"),
             )
 
-        gather_queries(0, 0, S2)
         for a in range(2):
             for b in range(2):
                 gather_keys(a, b)
+            if a == 0:
+                gather_queries(0, 0, S2)
 
         def bank(n):
             return psum.tile([P, BANK], F32, name="bank%d" % n)

@@ -119,8 +119,8 @@ def tile_list_decayed_key_read_kernel(
         load_key_half(1, 0)
         place_scale_rows(0)
         load_key_half(1, 1)
-        load_words(query_table[1], tab2_words[1], slice(0, T2))
         place_scale_rows(1)
+        load_words(query_table[1], tab2_words[1], slice(0, T2))
         def load_wg(b):
             nc.sync.dma_start(
                 out=wg_raw[b][:], in_=wg[b * PASS : (b + 1) * PASS, :].rearrange("(p t) n -> p t n", t=PACK)

@@ -44,7 +44,8 @@ def tile_list_decayed_key_read_kernel(
         query_scale_table = keep.tile([P, T2 // 4], I32, name="query_scale_table", align_bytes=64)
         w4_codes = keep.tile([P, 2, N // 2], I32, name="w4_codes", align_bytes=64)
         w4_plane = keep.tile([P, 2, N // 4], I32, name="w4_plane", align_bytes=64)
-        wg_raw = [keep.tile([P, PACK, N], F32, name="wg_raw%d" % b, align_bytes=64) for b in range(2)]
+        wg_raw0 = keep.tile([P, PACK, N], F32, name="wg_raw0", align_bytes=64)
+        wg_raw1 = [keep.tile([P, PACK, N // 2], F32, name="wg_raw1_%d" % c, align_bytes=64) for c in range(2)]
         decay = keep.tile([P, 2, PACK], F32, name="decay")
         log_decay = keep.tile([P, 2, PACK], F32, name="log_decay")
 
@@ -116,30 +117,33 @@ def tile_list_decayed_key_read_kernel(
                     in_=dense_planes[first : first + 13 : 4, :].bitcast(I32),
                 )
 
-        load_key_half(1, 0)
-        place_scale_rows(0)
-        load_key_half(1, 1)
-        place_scale_rows(1)
         load_words(query_table[1], tab2_words[1], slice(0, T2))
-        def load_wg(b):
+        place_scale_rows(0)
+        load_key_half(1, 0)
+        place_scale_rows(1)
+        load_key_half(1, 1)
+
+        def load_wg(tile, b, cols):
             nc.sync.dma_start(
-                out=wg_raw[b][:], in_=wg[b * PASS : (b + 1) * PASS, :].rearrange("(p t) n -> p t n", t=PACK)
+                out=tile[:], in_=wg[b * PASS : (b + 1) * PASS, :].rearrange("(p t) n -> p t n", t=PACK)[:, :, cols]
             )
 
-        load_wg(0)
+        load_wg(wg_raw0, 0, slice(0, N))
+        for c in range(2):
+            load_wg(wg_raw1[c], 1, slice(c * N // 2, (c + 1) * N // 2))
         nc.sync.dma_start(out=w4_codes[:], in_=w4_words.bitcast(I32).rearrange("a p c -> p a c"))
-        load_wg(1)
         for q in range(4):
             nc.sync.dma_start(
                 out=w4_plane[32 * q : 32 * q + 4, :, :],
                 in_=w4_scales.bitcast(I32)[:, 4 * q : 4 * q + 4, :].rearrange("a r n -> r a n"),
             )
 
+        for b in range(2):
+            gather_keys(0, b)
         for a in range(2):
-            for b in range(2):
-                gather_keys(a, b)
-            if a == 0:
-                gather_queries(0, 0, S2)
+            gather_queries(a, 0, S2)
+        for b in range(2):
+            gather_keys(1, b)
 
         def bank(n):
             return psum.tile([P, BANK], F32, name="bank%d" % n)
@@ -170,8 +174,6 @@ def tile_list_decayed_key_read_kernel(
         scores = [bank(n) for n in range(8)]
         for n in range(8):
             score_pass(scores[n], 0, n, 0)
-        for first, last in ((0, BANK // 2), (BANK // 2, BANK), (BANK, S2)):
-            gather_queries(1, first, last)
 
         def exponentials(accs, b):
             rows = ring.tile([P, PACK, BANK], BF16, name="rows", align_bytes=64)
@@ -186,17 +188,16 @@ def tile_list_decayed_key_read_kernel(
             interleave(copy, grouped[:], rows[:, :, first:last])
             return grouped
 
-        for first in (0, BANK // 2):
-            for n in range(4):
-                score_pass(scores[n], 1, n, 0, first, first + BANK // 2)
-        for n in range(4, 8):
+        for n in range(8):
             score_pass(scores[n], 1, n, 0)
         rows = {}
         for b in range(2):
             rows[0, b] = exponentials(scores, b)
-        wg_grouped = pack_rows(wg_raw[0], "grouped0")
-        grouped = pack_rows(rows[0, 0], "wg_raw0")
+        wg_grouped = pack_rows(wg_raw0, "grouped0")
         quantize(wg_codes[:, 0, :], wg_plane[:, 0, :], wg_grouped)
+        grouped = pack_rows(rows[0, 0], "grouped0")
+        wg_grouped = keep.tile([P, N, PACK], BF16, name="wg_grouped", align_bytes=64)
+        interleave(nc.vector.tensor_copy, wg_grouped[:, : N // 2, :], wg_raw1[0][:])
         quantize(p_codes[0][:, 0, :], p_plane[0][:, 0, :], grouped)
 
         scores = [bank(n) for n in range(8)]
@@ -205,13 +206,13 @@ def tile_list_decayed_key_read_kernel(
                 score_pass(scores[n], a, n, 1)
         for b in range(2):
             rows[1, b] = exponentials(scores, b)
-        grouped = pack_rows(rows[0, 1], "grouped0")
-        wg_grouped = pack_rows(wg_raw[1], "wg_raw0")
+        grouped = pack_rows(rows[0, 1], "grouped2")
+        interleave(nc.vector.tensor_copy, wg_grouped[:, N // 2 :, :], wg_raw1[1][:])
         quantize(p_codes[0][:, 1, :], p_plane[0][:, 1, :], grouped)
         quantize(wg_codes[:, 1, :], wg_plane[:, 1, :], wg_grouped)
         grouped = pack_rows(rows[1, 0], "grouped0")
         left = pack_rows(rows[1, 1], "grouped1", nc.scalar.copy, 0, 256)
-        right = pack_rows(rows[1, 1], "wg_raw0", nc.vector.tensor_copy, 256, BANK)
+        right = pack_rows(rows[1, 1], "grouped2", nc.vector.tensor_copy, 256, BANK)
         quantize(p_codes[1][:, 0, :], p_plane[1][:, 0, :], grouped)
         quantize(p_codes[1][:, 1, :256], p_plane[1][:, 1, :256], left)
         quantize(p_codes[1][:, 1, 256:], p_plane[1][:, 1, 256:], right)
@@ -254,13 +255,15 @@ def tile_list_decayed_key_read_kernel(
                 )
 
         reads = [bank(n) for n in range(8)]
+        for b in range(2):
+            for n in range(4):
+                gate_pass(reads[n], n, 0, b)
         for n in range(4):
             for b in range(2):
-                gate_pass(reads[2 * n], n, 0, b)
-                value_pass(reads[2 * n + 1], n, 0, b)
+                value_pass(reads[4 + n], n, 0, b)
         for n in range(4):
-            finish(reads[2 * n], reads[2 * n + 1], n, 0, 1)
-        reads = [bank(n) for n in range(8)]
+            finish(reads[n], reads[4 + n], n, 0, 1)
+        reads = [bank(n) for n in (0, 1, 4, 2, 5, 3, 6, 7)]
         for n in range(4):
             for b in range(2):
                 gate_pass(reads[2 * n], n, 1, b)

@@ -22,6 +22,7 @@ PASS = P * PACK
 BANK = 512
 PLANE_ROW = (0, 4)
 DENSE = 96
+SHARE = 128
 
 
 def tile_list_decayed_key_read_kernel(
@@ -38,18 +39,18 @@ def tile_list_decayed_key_read_kernel(
         key_list = lists.tile([P, S // 16], U16, name="key_list")
         query_list = lists.tile([P, S2 // 16], U16, name="query_list")
 
-        key_table = [keep.tile([P, T], I32, name="key_table%d" % a, align_bytes=64) for a in range(2)]
-        query_table = [keep.tile([P, T2], I32, name="query_table%d" % a, align_bytes=64) for a in range(2)]
-        key_scale_table = keep.tile([P, T // 4], I32, name="key_scale_table", align_bytes=64)
-        query_scale_table = keep.tile([P, T2 // 4], I32, name="query_scale_table", align_bytes=64)
-        w4_codes = keep.tile([P, 2, N // 2], I32, name="w4_codes", align_bytes=64)
-        w4_plane = keep.tile([P, 2, N // 4], I32, name="w4_plane", align_bytes=64)
-        wg_raw0 = keep.tile([P, PACK, N], F32, name="wg_raw0", align_bytes=64)
-        wg_raw1 = [keep.tile([P, PACK, N // 2], F32, name="wg_raw1_%d" % c, align_bytes=64) for c in range(2)]
+        key_table = [keep.tile([P, T], I32, name="key_table%d" % a, align_bytes=256) for a in range(2)]
+        query_table = [keep.tile([P, T2], I32, name="query_table%d" % a, align_bytes=256) for a in range(2)]
+        key_scale_table = keep.tile([P, T // 4], I32, name="key_scale_table", align_bytes=256)
+        query_scale_table = keep.tile([P, T2 // 4], I32, name="query_scale_table", align_bytes=256)
+        w4_codes = keep.tile([P, 2, N // 2], I32, name="w4_codes", align_bytes=256)
+        w4_plane = keep.tile([P, 2, N // 4], I32, name="w4_plane", align_bytes=256)
+        wg_raw0 = keep.tile([P, PACK, N], F32, name="wg_raw0", align_bytes=256)
+        wg_raw1 = [keep.tile([P, PACK, N // 2], F32, name="wg_raw1_%d" % c, align_bytes=256) for c in range(2)]
         decay = keep.tile([P, 2, PACK], F32, name="decay")
         log_decay = keep.tile([P, 2, PACK], F32, name="log_decay")
 
-        planes = [keep.tile([P, (S + S2) // 4], I32, name="planes%d" % a, align_bytes=64) for a in range(2)]
+        planes = [keep.tile([P, (S + S2) // 4], I32, name="planes%d" % a, align_bytes=256) for a in range(2)]
         nc.vector.memset(query_scale_table[0:DENSE, :], 0)
         nc.vector.memset(key_scale_table[0:DENSE, :], 0)
         nc.vector.memset(planes[0][:], 0)
@@ -78,11 +79,11 @@ def tile_list_decayed_key_read_kernel(
         warm = keep.tile([P, 1], F32, name="warm")
         nc.scalar.activation(out=warm[:], in_=log_decay[:, 0, 0:1], func=ACT.Exp)
 
-        keys = [keep.tile([P, S], U32, name="keys%d" % a, align_bytes=64) for a in range(2)]
-        queries = [keep.tile([P, S2], U32, name="queries%d" % a, align_bytes=64) for a in range(2)]
-        key_plane_listed = keep.tile([P, S], U8, name="key_plane_listed", align_bytes=64)
-        query_plane_listed = keep.tile([P, S2], U8, name="query_plane_listed", align_bytes=64)
-        dense_planes = keep.tile([P, S + S2], U8, name="dense_planes", align_bytes=64)
+        keys = [keep.tile([P, S], U32, name="keys%d" % a, align_bytes=256) for a in range(2)]
+        queries = [keep.tile([P, S2], U32, name="queries%d" % a, align_bytes=256) for a in range(2)]
+        key_plane_listed = keep.tile([P, S], U8, name="key_plane_listed", align_bytes=256)
+        query_plane_listed = keep.tile([P, S2], U8, name="query_plane_listed", align_bytes=256)
+        dense_planes = keep.tile([P, S + S2], U8, name="dense_planes", align_bytes=256)
 
         def half(h):
             return slice(h * BANK, (h + 1) * BANK)
@@ -166,17 +167,17 @@ def tile_list_decayed_key_read_kernel(
         def quantize(codes, plane, grouped):
             nc.vector.quantize_mx(out=codes.bitcast(FP8X4), scales=plane, in_=grouped[:].rearrange("p n t -> p (n t)"))
 
-        wg_codes = keep.tile([P, 2, N], U32, name="wg_codes", align_bytes=64)
-        wg_plane = keep.tile([P, 2, N], U8, name="wg_plane", align_bytes=64)
-        p_codes = [keep.tile([P, 2, BANK], U32, name="p_codes%d" % h, align_bytes=64) for h in range(2)]
-        p_plane = [keep.tile([P, 2, BANK], U8, name="p_plane%d" % h, align_bytes=64) for h in range(2)]
+        wg_codes = keep.tile([P, 2, N], U32, name="wg_codes", align_bytes=256)
+        wg_plane = keep.tile([P, 2, N], U8, name="wg_plane", align_bytes=256)
+        p_codes = [keep.tile([P, 2, BANK], U32, name="p_codes%d" % h, align_bytes=256) for h in range(2)]
+        p_plane = [keep.tile([P, 2, BANK], U8, name="p_plane%d" % h, align_bytes=256) for h in range(2)]
 
         scores = [bank(n) for n in range(8)]
         for n in range(8):
             score_pass(scores[n], 0, n, 0)
 
         def exponentials(accs, b):
-            rows = ring.tile([P, PACK, BANK], BF16, name="rows", align_bytes=64)
+            rows = ring.tile([P, PACK, BANK], BF16, name="rows", align_bytes=256)
             for t in range(PACK):
                 nc.scalar.activation(
                     out=rows[:, t, :], in_=accs[PACK * b + t][:], func=ACT.Exp, bias=log_decay[:, b, t : t + 1]
@@ -184,7 +185,7 @@ def tile_list_decayed_key_read_kernel(
             return rows
 
         def pack_rows(rows, slot, copy=nc.vector.tensor_copy, first=0, last=BANK):
-            grouped = keep.tile([P, last - first, PACK], BF16, name=slot, align_bytes=64)
+            grouped = keep.tile([P, last - first, PACK], BF16, name=slot, align_bytes=256)
             interleave(copy, grouped[:], rows[:, :, first:last])
             return grouped
 
@@ -196,7 +197,7 @@ def tile_list_decayed_key_read_kernel(
         wg_grouped = pack_rows(wg_raw0, "grouped0")
         quantize(wg_codes[:, 0, :], wg_plane[:, 0, :], wg_grouped)
         grouped = pack_rows(rows[0, 0], "grouped0")
-        wg_grouped = keep.tile([P, N, PACK], BF16, name="wg_grouped", align_bytes=64)
+        wg_grouped = keep.tile([P, N, PACK], BF16, name="wg_grouped", align_bytes=256)
         interleave(nc.vector.tensor_copy, wg_grouped[:, : N // 2, :], wg_raw1[0][:])
         quantize(p_codes[0][:, 0, :], p_plane[0][:, 0, :], grouped)
 
@@ -211,11 +212,7 @@ def tile_list_decayed_key_read_kernel(
         quantize(p_codes[0][:, 1, :], p_plane[0][:, 1, :], grouped)
         quantize(wg_codes[:, 1, :], wg_plane[:, 1, :], wg_grouped)
         grouped = pack_rows(rows[1, 0], "grouped0")
-        left = pack_rows(rows[1, 1], "grouped1", nc.scalar.copy, 0, 256)
-        right = pack_rows(rows[1, 1], "grouped2", nc.vector.tensor_copy, 256, BANK)
         quantize(p_codes[1][:, 0, :], p_plane[1][:, 0, :], grouped)
-        quantize(p_codes[1][:, 1, :256], p_plane[1][:, 1, :256], left)
-        quantize(p_codes[1][:, 1, 256:], p_plane[1][:, 1, 256:], right)
 
         def gate_pass(gate, n, h, b):
             cols = slice(n * P, (n + 1) * P)
@@ -241,18 +238,17 @@ def tile_list_decayed_key_read_kernel(
                 stop=(b == 1),
             )
 
-        def finish(gate, value, n, h, pieces):
-            width = BANK // pieces
-            for c in range(0, BANK, width):
-                damp = tail.tile([P, width], F32, name="damp")
-                nc.scalar.activation(out=damp[:], in_=gate[:, c : c + width], func=ACT.Tanh)
-                result = tail.tile([P, width], F32, name="result")
-                nc.vector.scalar_tensor_tensor(
-                    out=result[:], in0=damp[:], scalar=1.0, in1=value[:, c : c + width], op0=ALU.add, op1=ALU.mult
-                )
-                nc.sync.dma_start(
-                    out=out[n * P : (n + 1) * P, h * BANK + c : h * BANK + c + width], in_=result[:]
-                )
+        def damping(gate, first, last):
+            damp = tail.tile([P, last - first], F32, name="damp")
+            nc.scalar.activation(out=damp[:], in_=gate[:, first:last], func=ACT.Tanh)
+            return damp
+
+        def finish(damp, value, n, h, first, last):
+            result = tail.tile([P, last - first], F32, name="result")
+            nc.vector.scalar_tensor_tensor(
+                out=result[:], in0=damp[:], scalar=1.0, in1=value[:, first:last], op0=ALU.add, op1=ALU.mult
+            )
+            nc.sync.dma_start(out=out[n * P : (n + 1) * P, h * BANK + first : h * BANK + last], in_=result[:])
 
         reads = [bank(n) for n in range(8)]
         for b in range(2):
@@ -261,13 +257,21 @@ def tile_list_decayed_key_read_kernel(
         for n in range(4):
             for b in range(2):
                 value_pass(reads[4 + n], n, 0, b)
-        for n in range(4):
-            finish(reads[n], reads[4 + n], n, 0, 1)
-        reads = [bank(n) for n in (0, 1, 4, 2, 5, 3, 6, 7)]
+        damp = damping(reads[0], 0, BANK)
+        grouped = keep.tile([P, BANK, PACK], BF16, name="grouped2", align_bytes=256)
+        interleave(nc.scalar.copy, grouped[:, :SHARE, :], rows[1, 1][:, :, :SHARE])
+        interleave(nc.vector.tensor_copy, grouped[:, SHARE:, :], rows[1, 1][:, :, SHARE:])
+        quantize(p_codes[1][:, 1, :], p_plane[1][:, 1, :], grouped)
+        finish(damp, reads[4], 0, 0, 0, BANK)
+        for n in range(1, 4):
+            finish(damping(reads[n], 0, BANK), reads[4 + n], n, 0, 0, BANK)
+        reads = [bank(n) for n in (0, 1, 2, 4, 3, 5, 6, 7)]
         for n in range(4):
             for b in range(2):
                 gate_pass(reads[2 * n], n, 1, b)
             for b in range(2):
                 value_pass(reads[2 * n + 1], n, 1, b)
         for n in range(4):
-            finish(reads[2 * n], reads[2 * n + 1], n, 1, 2 if n == 3 else 1)
+            width = BANK // 2 if n == 3 else BANK
+            for first in range(0, BANK, width):
+                finish(damping(reads[2 * n], first, first + width), reads[2 * n + 1], n, 1, first, first + width)

@@ -162,7 +162,8 @@ def tile_list_decayed_key_read_kernel(
             )
 
         def interleave(copy, dst, src):
-            copy(out=dst.rearrange("p (c i) t -> p c t i", i=4), in_=src.rearrange("p t (c i) -> p c t i", i=4))
+            run = 4 if src.dtype == F32 else 8
+            copy(out=dst.rearrange("p (c i) t -> p c t i", i=run), in_=src.rearrange("p t (c i) -> p c t i", i=run))
 
         def quantize(codes, plane, grouped):
             nc.vector.quantize_mx(out=codes.bitcast(FP8X4), scales=plane, in_=grouped[:].rearrange("p n t -> p (n t)"))

@@ -22,6 +22,7 @@ PASS = P * PACK
 BANK = 512
 PLANE_ROW = (0, 4)
 DENSE = 96
+HEAD = 192
 SHARE = 128
 
 
@@ -32,7 +33,6 @@ def tile_list_decayed_key_read_kernel(
     with ExitStack() as ctx:
         lists = ctx.enter_context(tc.tile_pool(name="lists", bufs=1))
         keep = ctx.enter_context(tc.tile_pool(name="keep", bufs=1))
-        ring = ctx.enter_context(tc.tile_pool(name="ring", bufs=4))
         tail = ctx.enter_context(tc.tile_pool(name="tail", bufs=8))
         psum = ctx.enter_context(tc.psum_pool(name="psum", bufs=1))
 
@@ -45,17 +45,21 @@ def tile_list_decayed_key_read_kernel(
         query_scale_table = keep.tile([P, T2 // 4], I32, name="query_scale_table", align_bytes=256)
         w4_codes = keep.tile([P, 2, N // 2], I32, name="w4_codes", align_bytes=256)
         w4_plane = keep.tile([P, 2, N // 4], I32, name="w4_plane", align_bytes=256)
-        wg_raw0 = keep.tile([P, PACK, N], F32, name="wg_raw0", align_bytes=256)
-        wg_raw1 = [keep.tile([P, PACK, N // 2], F32, name="wg_raw1_%d" % c, align_bytes=256) for c in range(2)]
+        wg_cuts = {(0, 0): (0, HEAD), (0, 1): (HEAD, N), (1, 0): (0, N // 2), (1, 1): (N // 2, N)}
+        wg_raw = {
+            (b, c): keep.tile([P, PACK, last - first], F32, name="wg_raw%d%d" % (b, c), align_bytes=256)
+            for (b, c), (first, last) in wg_cuts.items()
+        }
         decay = keep.tile([P, 2, PACK], F32, name="decay")
-        log_decay = keep.tile([P, 2, PACK], F32, name="log_decay")
+        slots = {(0, 0): "first_bias", (0, 1): "second_bias", (1, 0): "wg_codes11", (1, 1): "last_bias"}
+        log_decay = {hb: keep.tile([P, PACK], F32, name=slot, align_bytes=256) for hb, slot in slots.items()}
 
         planes = [keep.tile([P, (S + S2) // 4], I32, name="planes%d" % a, align_bytes=256) for a in range(2)]
         nc.vector.memset(query_scale_table[0:DENSE, :], 0)
         nc.vector.memset(key_scale_table[0:DENSE, :], 0)
-        nc.vector.memset(planes[0][:], 0)
-        nc.vector.memset(planes[1][:], 0)
-        nc.vector.memset(w4_plane[:], 0)
+        nc.gpsimd.memset(planes[0][:], 0)
+        nc.gpsimd.memset(planes[1][:], 0)
+        nc.gpsimd.memset(w4_plane[:], 0)
 
         def load_words(tile, words, cols):
             nc.sync.dma_start(out=tile[:, cols], in_=words.rearrange("p t i -> p (t i)").bitcast(I32)[:, cols])
@@ -75,9 +79,13 @@ def tile_list_decayed_key_read_kernel(
         load_words(query_table[0], tab2_words[0], slice(0, T2))
         nc.scalar.dma_start(out=decay[:], in_=dec.rearrange("(b p t) -> p b t", b=2, t=PACK))
 
-        nc.scalar.activation(out=log_decay[:], in_=decay[:], func=ACT.Ln, scale=0.5)
+        for h in range(2):
+            for b in range(2):
+                nc.scalar.activation(out=log_decay[h, b][:], in_=decay[:, b, :], func=ACT.Ln, scale=0.5)
+        opening_bias = keep.tile([P, 1], F32, name="rows01", align_bytes=256)
+        nc.scalar.activation(out=opening_bias[:], in_=decay[:, 0, 0:1], func=ACT.Ln, scale=0.5)
         warm = keep.tile([P, 1], F32, name="warm")
-        nc.scalar.activation(out=warm[:], in_=log_decay[:, 0, 0:1], func=ACT.Exp)
+        nc.scalar.activation(out=warm[:], in_=opening_bias[:], func=ACT.Exp)
 
         keys = [keep.tile([P, S], U32, name="keys%d" % a, align_bytes=256) for a in range(2)]
         queries = [keep.tile([P, S2], U32, name="queries%d" % a, align_bytes=256) for a in range(2)]
@@ -121,17 +129,17 @@ def tile_list_decayed_key_read_kernel(
         load_words(query_table[1], tab2_words[1], slice(0, T2))
         place_scale_rows(0)
         load_key_half(1, 0)
-        place_scale_rows(1)
         load_key_half(1, 1)
+        place_scale_rows(1)
 
-        def load_wg(tile, b, cols):
-            nc.sync.dma_start(
-                out=tile[:], in_=wg[b * PASS : (b + 1) * PASS, :].rearrange("(p t) n -> p t n", t=PACK)[:, :, cols]
-            )
+        def load_wg(b, c):
+            rows_of_pass = wg[b * PASS : (b + 1) * PASS, :].rearrange("(p t) n -> p t n", t=PACK)
+            nc.sync.dma_start(out=wg_raw[b, c][:], in_=rows_of_pass[:, :, slice(*wg_cuts[b, c])])
 
-        load_wg(wg_raw0, 0, slice(0, N))
-        for c in range(2):
-            load_wg(wg_raw1[c], 1, slice(c * N // 2, (c + 1) * N // 2))
+        load_wg(0, 0)
+        load_wg(0, 1)
+        load_wg(1, 0)
+        load_wg(1, 1)
         nc.sync.dma_start(out=w4_codes[:], in_=w4_words.bitcast(I32).rearrange("a p c -> p a c"))
         for q in range(4):
             nc.sync.dma_start(
@@ -166,9 +174,9 @@ def tile_list_decayed_key_read_kernel(
             copy(out=dst.rearrange("p (c i) t -> p c t i", i=run), in_=src.rearrange("p t (c i) -> p c t i", i=run))
 
         def quantize(codes, plane, grouped):
-            nc.vector.quantize_mx(out=codes.bitcast(FP8X4), scales=plane, in_=grouped[:].rearrange("p n t -> p (n t)"))
+            nc.vector.quantize_mx(out=codes.bitcast(FP8X4), scales=plane, in_=grouped.rearrange("p n t -> p (n t)"))
 
-        wg_codes = keep.tile([P, 2, N], U32, name="wg_codes", align_bytes=256)
+        wg_codes = {}
         wg_plane = keep.tile([P, 2, N], U8, name="wg_plane", align_bytes=256)
         p_codes = [keep.tile([P, 2, BANK], U32, name="p_codes%d" % h, align_bytes=256) for h in range(2)]
         p_plane = [keep.tile([P, 2, BANK], U8, name="p_plane%d" % h, align_bytes=256) for h in range(2)]
@@ -177,49 +185,69 @@ def tile_list_decayed_key_read_kernel(
         for n in range(8):
             score_pass(scores[n], 0, n, 0)
 
-        def exponentials(accs, b):
-            rows = ring.tile([P, PACK, BANK], BF16, name="rows", align_bytes=256)
-            for t in range(PACK):
-                nc.scalar.activation(
-                    out=rows[:, t, :], in_=accs[PACK * b + t][:], func=ACT.Exp, bias=log_decay[:, b, t : t + 1]
-                )
+        def exponentials(accs, h, b):
+            rows = keep.tile([P, PACK, BANK], BF16, name="rows%d%d" % (h, b) if h + b else "wg_raw00", align_bytes=256)
+            width = BANK // 2 if b == 1 else BANK
+            for first in range(0, BANK, width):
+                for t in range(PACK):
+                    nc.scalar.activation(
+                        out=rows[:, t, first : first + width],
+                        in_=accs[PACK * b + t][:, first : first + width],
+                        func=ACT.Exp,
+                        bias=log_decay[h, b][:, t : t + 1] if h + b + t else opening_bias[:],
+                    )
             return rows
 
-        def pack_rows(rows, slot, copy=nc.vector.tensor_copy, first=0, last=BANK):
-            grouped = keep.tile([P, last - first, PACK], BF16, name=slot, align_bytes=256)
-            interleave(copy, grouped[:], rows[:, :, first:last])
+        def group(src, slot, copy=nc.vector.tensor_copy):
+            grouped = keep.tile([P, src.shape[2], PACK], BF16, name=slot, align_bytes=256)
+            interleave(copy, grouped[:], src)
             return grouped
 
+        def quantize_wg(b, c, grouped):
+            wg_codes[b, c] = keep.tile([P, N // 2], U32, name="wg_codes%d%d" % (b, c), align_bytes=256)
+            quantize(wg_codes[b, c][:], wg_plane[:, b, c * N // 2 : (c + 1) * N // 2], grouped[:])
+
+        def quantize_p(h, b, grouped):
+            quantize(p_codes[h][:, b, :], p_plane[h][:, b, :], grouped[:])
+
+        wg_first = keep.tile([P, N, PACK], BF16, name="wg_first", align_bytes=256)
+        interleave(nc.scalar.copy, wg_first[:, :HEAD, :], wg_raw[0, 0][:])
         for n in range(8):
             score_pass(scores[n], 1, n, 0)
         rows = {}
         for b in range(2):
-            rows[0, b] = exponentials(scores, b)
-        wg_grouped = pack_rows(wg_raw0, "grouped0")
-        quantize(wg_codes[:, 0, :], wg_plane[:, 0, :], wg_grouped)
-        grouped = pack_rows(rows[0, 0], "grouped0")
-        wg_grouped = keep.tile([P, N, PACK], BF16, name="wg_grouped", align_bytes=256)
-        interleave(nc.vector.tensor_copy, wg_grouped[:, : N // 2, :], wg_raw1[0][:])
-        quantize(p_codes[0][:, 0, :], p_plane[0][:, 0, :], grouped)
-
+            rows[0, b] = exponentials(scores, 0, b)
         scores = [bank(n) for n in range(8)]
         for n in range(8):
             for a in range(2):
                 score_pass(scores[n], a, n, 1)
         for b in range(2):
-            rows[1, b] = exponentials(scores, b)
-        grouped = pack_rows(rows[0, 1], "grouped2")
-        interleave(nc.vector.tensor_copy, wg_grouped[:, N // 2 :, :], wg_raw1[1][:])
-        quantize(p_codes[0][:, 1, :], p_plane[0][:, 1, :], grouped)
-        quantize(wg_codes[:, 1, :], wg_plane[:, 1, :], wg_grouped)
-        grouped = pack_rows(rows[1, 0], "grouped0")
-        quantize(p_codes[1][:, 0, :], p_plane[1][:, 0, :], grouped)
+            rows[1, b] = exponentials(scores, 1, b)
+
+        interleave(nc.vector.tensor_copy, wg_first[:, HEAD:, :], wg_raw[0, 1][:])
+        wg_left = group(wg_raw[1, 0][:], "wg_grouped2")
+        first_codes = keep.tile([P, N], U32, name="first_codes", align_bytes=256)
+        quantize(first_codes[:], wg_plane[:, 0, :], wg_first[:])
+        for c in range(2):
+            wg_codes[0, c] = first_codes[:, c * N // 2 : (c + 1) * N // 2]
+        quantize_wg(1, 0, wg_left)
+        halves = [slice(c * BANK // 2, (c + 1) * BANK // 2) for c in range(2)]
+        grouped = group(rows[0, 0][:], "p_grouped0")
+        left = group(rows[0, 1][:, :, halves[0]], "p_left")
+        quantize_p(0, 0, grouped)
+        right = group(rows[0, 1][:, :, halves[1]], "p_right")
+        quantize(p_codes[0][:, 1, halves[0]], p_plane[0][:, 1, halves[0]], left[:])
+        quantize(p_codes[0][:, 1, halves[1]], p_plane[0][:, 1, halves[1]], right[:])
+        wg_right = group(wg_raw[1, 1][:], "p_left")
+        grouped = group(rows[1, 0][:], "p_grouped2")
+        quantize_wg(1, 1, wg_right)
+        quantize_p(1, 0, grouped)
 
         def gate_pass(gate, n, h, b):
             cols = slice(n * P, (n + 1) * P)
             nc.tensor.matmul_mx(
                 out=gate[:],
-                lhsT=wg_codes[:, b, cols].bitcast(FP8X4),
+                lhsT=wg_codes[b, n // 2][:, n % 2 * P : (n % 2 + 1) * P].bitcast(FP8X4),
                 lhsT_scale=wg_plane[:, b, cols],
                 rhs=p_codes[h][:, b, :].bitcast(FP8X4),
                 rhs_scale=p_plane[h][:, b, :],
@@ -227,14 +255,14 @@ def tile_list_decayed_key_read_kernel(
                 stop=(b == 1),
             )
 
-        def value_pass(value, n, h, b):
+        def value_pass(value, n, h, b, first=0, last=BANK):
             cols = slice(n * P, (n + 1) * P)
             nc.tensor.matmul_mx(
-                out=value[:],
+                out=value[:, first:last],
                 lhsT=w4_codes[:, b, n * (P // 2) : (n + 1) * (P // 2)].bitcast(FP4X4),
                 lhsT_scale=w4_plane[:, b, :].bitcast(U8)[:, cols],
-                rhs=p_codes[h][:, b, :].bitcast(FP8X4),
-                rhs_scale=p_plane[h][:, b, :],
+                rhs=p_codes[h][:, b, first:last].bitcast(FP8X4),
+                rhs_scale=p_plane[h][:, b, first:last],
                 start=(b == 0),
                 stop=(b == 1),
             )
@@ -245,34 +273,57 @@ def tile_list_decayed_key_read_kernel(
             return damp
 
         def finish(damp, value, n, h, first, last):
-            result = tail.tile([P, last - first], F32, name="result")
+            if n + h == 0:
+                result = keep.tile([P, BANK], F32, name="rows11", align_bytes=256)
+            else:
+                result = tail.tile([P, last - first], F32, name="result")
             nc.vector.scalar_tensor_tensor(
-                out=result[:], in0=damp[:], scalar=1.0, in1=value[:, first:last], op0=ALU.add, op1=ALU.mult
+                out=result[:], in0=damp[:], scalar=1.0, in1=value, op0=ALU.add, op1=ALU.mult
             )
             nc.sync.dma_start(out=out[n * P : (n + 1) * P, h * BANK + first : h * BANK + last], in_=result[:])
 
-        reads = [bank(n) for n in range(8)]
+        gates = [bank(n) for n in (0, 1, 6, 7)]
+        values = [bank(n) for n in (2, 3, 4, 5)]
+        gate_pass(gates[0], 0, 0, 0)
+        gate_pass(gates[1], 1, 0, 0)
+        value_pass(values[0], 0, 0, 0)
+        gate_pass(gates[0], 0, 0, 1)
+        value_pass(values[1], 1, 0, 0)
+        gate_pass(gates[1], 1, 0, 1)
+        for n in range(2):
+            value_pass(values[n], n, 0, 1)
+        for read_pass, accs in ((value_pass, values), (gate_pass, gates)):
+            for n in range(2, 4):
+                for b in range(2):
+                    read_pass(accs[n], n, 0, b)
+        left = group(rows[1, 1][:, :, halves[0]], "p_grouped0")
+        right = keep.tile([P, BANK // 2, PACK], BF16, name="p_right", align_bytes=256)
+        interleave(nc.scalar.copy, right[:, :SHARE, :], rows[1, 1][:, :, BANK // 2 : BANK // 2 + SHARE])
+        interleave(nc.vector.tensor_copy, right[:, SHARE:, :], rows[1, 1][:, :, BANK // 2 + SHARE :])
+        quantize(p_codes[1][:, 1, halves[0]], p_plane[1][:, 1, halves[0]], left[:])
+        quantize(p_codes[1][:, 1, halves[1]], p_plane[1][:, 1, halves[1]], right[:])
+        for n in range(4):
+            finish(damping(gates[n], 0, BANK), values[n][:], n, 0, 0, BANK)
+        gates = [bank(n) for n in (0, 6, 7, 4)]
+        values = [bank(n) for n in (1, 2, 3, 5)]
+        gate_pass(gates[0], 0, 1, 0)
+        value_pass(values[0], 0, 1, 0)
+        gate_pass(gates[0], 0, 1, 1)
+        value_pass(values[0], 0, 1, 1)
+        for n in range(1, 3):
+            for b in range(2):
+                gate_pass(gates[n], n, 1, b)
+            for b in range(2):
+                value_pass(values[n], n, 1, b)
+        finish(damping(gates[0], 0, BANK), values[0][:], 0, 1, 0, BANK)
         for b in range(2):
-            for n in range(4):
-                gate_pass(reads[n], n, 0, b)
-        for n in range(4):
+            gate_pass(gates[3], 3, 1, b)
+        last_values = [values[3], bank(0)]
+        for first in range(0, BANK, P):
             for b in range(2):
-                value_pass(reads[4 + n], n, 0, b)
-        damp = damping(reads[0], 0, BANK)
-        grouped = keep.tile([P, BANK, PACK], BF16, name="grouped2", align_bytes=256)
-        interleave(nc.scalar.copy, grouped[:, :SHARE, :], rows[1, 1][:, :, :SHARE])
-        interleave(nc.vector.tensor_copy, grouped[:, SHARE:, :], rows[1, 1][:, :, SHARE:])
-        quantize(p_codes[1][:, 1, :], p_plane[1][:, 1, :], grouped)
-        finish(damp, reads[4], 0, 0, 0, BANK)
-        for n in range(1, 4):
-            finish(damping(reads[n], 0, BANK), reads[4 + n], n, 0, 0, BANK)
-        reads = [bank(n) for n in (0, 1, 2, 4, 3, 5, 6, 7)]
-        for n in range(4):
-            for b in range(2):
-                gate_pass(reads[2 * n], n, 1, b)
-            for b in range(2):
-                value_pass(reads[2 * n + 1], n, 1, b)
-        for n in range(4):
-            width = BANK // 2 if n == 3 else BANK
-            for first in range(0, BANK, width):
-                finish(damping(reads[2 * n], first, first + width), reads[2 * n + 1], n, 1, first, first + width)
+                value_pass(last_values[first // (BANK // 2)], 3, 1, b, first, first + P)
+        for n in range(1, 3):
+            finish(damping(gates[n], 0, BANK), values[n][:], n, 1, 0, BANK)
+        for c in range(2):
+            first, last = c * BANK // 2, (c + 1) * BANK // 2
+            finish(damping(gates[3], first, last), last_values[c][:, first:last], 3, 1, first, last)

@@ -23,7 +23,8 @@ BANK = 512
 PLANE_ROW = (0, 4)
 DENSE = 96
 HEAD = 192
-SHARE = 128
+SHARE = 192
+LATE = 768
 
 
 def tile_list_decayed_key_read_kernel(
@@ -51,7 +52,7 @@ def tile_list_decayed_key_read_kernel(
             for (b, c), (first, last) in wg_cuts.items()
         }
         decay = keep.tile([P, 2, PACK], F32, name="decay")
-        slots = {(0, 0): "first_bias", (0, 1): "second_bias", (1, 0): "wg_codes11", (1, 1): "last_bias"}
+        slots = {(0, 0): "first_bias", (0, 1): "first_codes", (1, 0): "wg_codes11", (1, 1): "last_bias"}
         log_decay = {hb: keep.tile([P, PACK], F32, name=slot, align_bytes=256) for hb, slot in slots.items()}
 
         planes = [keep.tile([P, (S + S2) // 4], I32, name="planes%d" % a, align_bytes=256) for a in range(2)]
@@ -88,7 +89,7 @@ def tile_list_decayed_key_read_kernel(
         nc.scalar.activation(out=warm[:], in_=opening_bias[:], func=ACT.Exp)
 
         keys = [keep.tile([P, S], U32, name="keys%d" % a, align_bytes=256) for a in range(2)]
-        queries = [keep.tile([P, S2], U32, name="queries%d" % a, align_bytes=256) for a in range(2)]
+        queries = {}
         key_plane_listed = keep.tile([P, S], U8, name="key_plane_listed", align_bytes=256)
         query_plane_listed = keep.tile([P, S2], U8, name="query_plane_listed", align_bytes=256)
         dense_planes = keep.tile([P, S + S2], U8, name="dense_planes", align_bytes=256)
@@ -99,9 +100,10 @@ def tile_list_decayed_key_read_kernel(
         def list_half(tile, h):
             return tile[:, h * (BANK // 16) : (h + 1) * (BANK // 16)]
 
-        def gather_queries(a, first, last):
+        def gather_queries(a, first, last, slot):
+            queries[a, first] = keep.tile([P, last - first], U32, name=slot, align_bytes=256)
             nc.vector.tensor_copy(
-                queries[a][:, first:last], query_table[a][:].bitcast(U32).indirect(query_list[:, first // 16 : last // 16])
+                queries[a, first][:], query_table[a][:].bitcast(U32).indirect(query_list[:, first // 16 : last // 16])
             )
 
         def gather_keys(a, b):
@@ -139,31 +141,33 @@ def tile_list_decayed_key_read_kernel(
         load_wg(0, 0)
         load_wg(0, 1)
         load_wg(1, 0)
-        load_wg(1, 1)
         nc.sync.dma_start(out=w4_codes[:], in_=w4_words.bitcast(I32).rearrange("a p c -> p a c"))
         for q in range(4):
             nc.sync.dma_start(
                 out=w4_plane[32 * q : 32 * q + 4, :, :],
                 in_=w4_scales.bitcast(I32)[:, 4 * q : 4 * q + 4, :].rearrange("a r n -> r a n"),
             )
+        load_wg(1, 1)
 
         for b in range(2):
             gather_keys(0, b)
-        for a in range(2):
-            gather_queries(a, 0, S2)
+        gather_queries(0, 0, S2, "queries0")
+        gather_queries(1, 0, LATE, "queries1")
         for b in range(2):
             gather_keys(1, b)
+        gather_queries(1, LATE, S2, "dense_planes")
 
         def bank(n):
             return psum.tile([P, BANK], F32, name="bank%d" % n)
 
         def score_pass(acc, a, tile_index, h, first=0, last=BANK):
             cols = slice(tile_index * P, (tile_index + 1) * P)
+            start = LATE if a == 1 and h * BANK + first >= LATE else 0
             nc.tensor.matmul_mx(
                 out=acc[:, first:last],
                 lhsT=keys[a][:, cols].bitcast(FP8X4),
                 lhsT_scale=planes[a][PLANE_ROW[a] : P, :].bitcast(U8)[:, cols],
-                rhs=queries[a][:, h * BANK + first : h * BANK + last].bitcast(FP8X4),
+                rhs=queries[a, start][:, h * BANK + first - start : h * BANK + last - start].bitcast(FP8X4),
                 rhs_scale=planes[a][PLANE_ROW[a] : P, :].bitcast(U8)[:, S + h * BANK + first : S + h * BANK + last],
                 start=(a == 0),
                 stop=(a == 1 and last == BANK),
@@ -187,7 +191,7 @@ def tile_list_decayed_key_read_kernel(
 
         def exponentials(accs, h, b):
             rows = keep.tile([P, PACK, BANK], BF16, name="rows%d%d" % (h, b) if h + b else "wg_raw00", align_bytes=256)
-            width = BANK // 2 if b == 1 else BANK
+            width = BANK // 2 if (h, b) == (0, 1) else BANK
             for first in range(0, BANK, width):
                 for t in range(PACK):
                     nc.scalar.activation(
@@ -204,7 +208,7 @@ def tile_list_decayed_key_read_kernel(
             return grouped
 
         def quantize_wg(b, c, grouped):
-            wg_codes[b, c] = keep.tile([P, N // 2], U32, name="wg_codes%d%d" % (b, c), align_bytes=256)
+            wg_codes[b, c] = keep.tile([P, N // 2], U32, name="wg_codes11" if c else "rows01", align_bytes=256)
             quantize(wg_codes[b, c][:], wg_plane[:, b, c * N // 2 : (c + 1) * N // 2], grouped[:])
 
         def quantize_p(h, b, grouped):
@@ -219,18 +223,14 @@ def tile_list_decayed_key_read_kernel(
             rows[0, b] = exponentials(scores, 0, b)
         scores = [bank(n) for n in range(8)]
         for n in range(8):
-            for a in range(2):
-                score_pass(scores[n], a, n, 1)
+            score_pass(scores[n], 0, n, 1)
+            score_pass(scores[n], 1, n, 1, 0, LATE - BANK)
+            score_pass(scores[n], 1, n, 1, LATE - BANK, BANK)
         for b in range(2):
             rows[1, b] = exponentials(scores, 1, b)
 
         interleave(nc.vector.tensor_copy, wg_first[:, HEAD:, :], wg_raw[0, 1][:])
         wg_left = group(wg_raw[1, 0][:], "wg_grouped2")
-        first_codes = keep.tile([P, N], U32, name="first_codes", align_bytes=256)
-        quantize(first_codes[:], wg_plane[:, 0, :], wg_first[:])
-        for c in range(2):
-            wg_codes[0, c] = first_codes[:, c * N // 2 : (c + 1) * N // 2]
-        quantize_wg(1, 0, wg_left)
         halves = [slice(c * BANK // 2, (c + 1) * BANK // 2) for c in range(2)]
         grouped = group(rows[0, 0][:], "p_grouped0")
         left = group(rows[0, 1][:, :, halves[0]], "p_left")
@@ -238,10 +238,16 @@ def tile_list_decayed_key_read_kernel(
         right = group(rows[0, 1][:, :, halves[1]], "p_right")
         quantize(p_codes[0][:, 1, halves[0]], p_plane[0][:, 1, halves[0]], left[:])
         quantize(p_codes[0][:, 1, halves[1]], p_plane[0][:, 1, halves[1]], right[:])
+        first_codes = keep.tile([P, N], U32, name="first_codes", align_bytes=256)
+        quantize(first_codes[:], wg_plane[:, 0, :], wg_first[:])
+        for c in range(2):
+            wg_codes[0, c] = first_codes[:, c * N // 2 : (c + 1) * N // 2]
         wg_right = group(wg_raw[1, 1][:], "p_left")
+        quantize_wg(1, 0, wg_left)
         grouped = group(rows[1, 0][:], "p_grouped2")
         quantize_wg(1, 1, wg_right)
         quantize_p(1, 0, grouped)
+        left = group(rows[1, 1][:, :, halves[0]], "p_grouped0")
 
         def gate_pass(gate, n, h, b):
             cols = slice(n * P, (n + 1) * P)
@@ -282,21 +288,15 @@ def tile_list_decayed_key_read_kernel(
             )
             nc.sync.dma_start(out=out[n * P : (n + 1) * P, h * BANK + first : h * BANK + last], in_=result[:])
 
-        gates = [bank(n) for n in (0, 1, 6, 7)]
-        values = [bank(n) for n in (2, 3, 4, 5)]
-        gate_pass(gates[0], 0, 0, 0)
-        gate_pass(gates[1], 1, 0, 0)
-        value_pass(values[0], 0, 0, 0)
-        gate_pass(gates[0], 0, 0, 1)
-        value_pass(values[1], 1, 0, 0)
-        gate_pass(gates[1], 1, 0, 1)
-        for n in range(2):
-            value_pass(values[n], n, 0, 1)
-        for read_pass, accs in ((value_pass, values), (gate_pass, gates)):
-            for n in range(2, 4):
+        values = [bank(n) for n in range(4)]
+        gates = [bank(4 + n) for n in range(4)]
+        for b in range(2):
+            for n in range(2):
+                value_pass(values[n], n, 0, b)
+        for read_pass, accs, first in ((value_pass, values, 2), (gate_pass, gates, 0)):
+            for n in range(first, 4):
                 for b in range(2):
                     read_pass(accs[n], n, 0, b)
-        left = group(rows[1, 1][:, :, halves[0]], "p_grouped0")
         right = keep.tile([P, BANK // 2, PACK], BF16, name="p_right", align_bytes=256)
         interleave(nc.scalar.copy, right[:, :SHARE, :], rows[1, 1][:, :, BANK // 2 : BANK // 2 + SHARE])
         interleave(nc.vector.tensor_copy, right[:, SHARE:, :], rows[1, 1][:, :, BANK // 2 + SHARE :])
@@ -304,8 +304,8 @@ def tile_list_decayed_key_read_kernel(
         quantize(p_codes[1][:, 1, halves[1]], p_plane[1][:, 1, halves[1]], right[:])
         for n in range(4):
             finish(damping(gates[n], 0, BANK), values[n][:], n, 0, 0, BANK)
-        gates = [bank(n) for n in (0, 6, 7, 4)]
-        values = [bank(n) for n in (1, 2, 3, 5)]
+        gates = [bank(n) for n in (4, 0, 1, 2)]
+        values = [bank(n) for n in (5, 6, 7, 3)]
         gate_pass(gates[0], 0, 1, 0)
         value_pass(values[0], 0, 1, 0)
         gate_pass(gates[0], 0, 1, 1)
@@ -318,7 +318,7 @@ def tile_list_decayed_key_read_kernel(
         finish(damping(gates[0], 0, BANK), values[0][:], 0, 1, 0, BANK)
         for b in range(2):
             gate_pass(gates[3], 3, 1, b)
-        last_values = [values[3], bank(0)]
+        last_values = [values[3], bank(4)]
         for first in range(0, BANK, P):
             for b in range(2):
                 value_pass(last_values[first // (BANK // 2)], 3, 1, b, first, first + P)

@@ -23,7 +23,7 @@ BANK = 512
 PLANE_ROW = (0, 4)
 DENSE = 96
 HEAD = 192
-SHARE = 192
+OWN = 256
 LATE = 768
 
 
@@ -52,7 +52,7 @@ def tile_list_decayed_key_read_kernel(
             for (b, c), (first, last) in wg_cuts.items()
         }
         decay = keep.tile([P, 2, PACK], F32, name="decay")
-        slots = {(0, 0): "first_bias", (0, 1): "first_codes", (1, 0): "wg_codes11", (1, 1): "last_bias"}
+        slots = {(0, 0): "wg_left", (0, 1): "wg_codes10", (1, 0): "wg_codes11", (1, 1): "last_bias"}
         log_decay = {hb: keep.tile([P, PACK], F32, name=slot, align_bytes=256) for hb, slot in slots.items()}
 
         planes = [keep.tile([P, (S + S2) // 4], I32, name="planes%d" % a, align_bytes=256) for a in range(2)]
@@ -100,11 +100,13 @@ def tile_list_decayed_key_read_kernel(
         def list_half(tile, h):
             return tile[:, h * (BANK // 16) : (h + 1) * (BANK // 16)]
 
-        def gather_queries(a, first, last, slot):
-            queries[a, first] = keep.tile([P, last - first], U32, name=slot, align_bytes=256)
-            nc.vector.tensor_copy(
-                queries[a, first][:], query_table[a][:].bitcast(U32).indirect(query_list[:, first // 16 : last // 16])
-            )
+        def gather_queries(a, cuts, slot):
+            queries[a, cuts[0]] = keep.tile([P, cuts[-1] - cuts[0]], U32, name=slot, align_bytes=256)
+            for first, last in zip(cuts, cuts[1:]):
+                nc.vector.tensor_copy(
+                    queries[a, cuts[0]][:, first - cuts[0] : last - cuts[0]],
+                    query_table[a][:].bitcast(U32).indirect(query_list[:, first // 16 : last // 16]),
+                )
 
         def gather_keys(a, b):
             nc.vector.tensor_copy(
@@ -128,10 +130,10 @@ def tile_list_decayed_key_read_kernel(
                     in_=dense_planes[first : first + 13 : 4, :].bitcast(I32),
                 )
 
-        load_words(query_table[1], tab2_words[1], slice(0, T2))
-        place_scale_rows(0)
         load_key_half(1, 0)
+        place_scale_rows(0)
         load_key_half(1, 1)
+        load_words(query_table[1], tab2_words[1], slice(0, T2))
         place_scale_rows(1)
 
         def load_wg(b, c):
@@ -151,26 +153,24 @@ def tile_list_decayed_key_read_kernel(
 
         for b in range(2):
             gather_keys(0, b)
-        gather_queries(0, 0, S2, "queries0")
-        gather_queries(1, 0, LATE, "queries1")
+        gather_queries(0, (0, LATE, S2), "queries0")
         for b in range(2):
             gather_keys(1, b)
-        gather_queries(1, LATE, S2, "dense_planes")
+        gather_queries(1, (0, BANK // 2, BANK, S2), "queries1")
 
         def bank(n):
             return psum.tile([P, BANK], F32, name="bank%d" % n)
 
-        def score_pass(acc, a, tile_index, h, first=0, last=BANK):
+        def score_pass(acc, a, tile_index, h, first, last, opens, closes):
             cols = slice(tile_index * P, (tile_index + 1) * P)
-            start = LATE if a == 1 and h * BANK + first >= LATE else 0
             nc.tensor.matmul_mx(
-                out=acc[:, first:last],
+                out=acc,
                 lhsT=keys[a][:, cols].bitcast(FP8X4),
                 lhsT_scale=planes[a][PLANE_ROW[a] : P, :].bitcast(U8)[:, cols],
-                rhs=queries[a, start][:, h * BANK + first - start : h * BANK + last - start].bitcast(FP8X4),
+                rhs=queries[a, 0][:, h * BANK + first : h * BANK + last].bitcast(FP8X4),
                 rhs_scale=planes[a][PLANE_ROW[a] : P, :].bitcast(U8)[:, S + h * BANK + first : S + h * BANK + last],
-                start=(a == 0),
-                stop=(a == 1 and last == BANK),
+                start=opens,
+                stop=closes,
             )
 
         def interleave(copy, dst, src):
@@ -182,23 +182,33 @@ def tile_list_decayed_key_read_kernel(
 
         wg_codes = {}
         wg_plane = keep.tile([P, 2, N], U8, name="wg_plane", align_bytes=256)
-        p_codes = [keep.tile([P, 2, BANK], U32, name="p_codes%d" % h, align_bytes=256) for h in range(2)]
+        p_codes = {
+            hb: keep.tile([P, BANK], U32, name="p_codes%d%d" % hb, align_bytes=256) for hb in ((0, 0), (0, 1), (1, 0))
+        }
         p_plane = [keep.tile([P, 2, BANK], U8, name="p_plane%d" % h, align_bytes=256) for h in range(2)]
 
         scores = [bank(n) for n in range(8)]
-        for n in range(8):
-            score_pass(scores[n], 0, n, 0)
+        QUARTER = BANK // 2
+
+        def opening_scores(n, c):
+            return scores[2 * c + n // 2][:, n % 2 * QUARTER : (n % 2 + 1) * QUARTER]
+
+        for c in range(2):
+            for n in range(PACK):
+                score_pass(opening_scores(n, c), 0, n, 0, c * QUARTER, (c + 1) * QUARTER, n % 2 == 0, False)
+        for n in range(PACK, 2 * PACK):
+            score_pass(scores[n][:], 0, n, 0, 0, BANK, True, False)
 
         def exponentials(accs, h, b):
-            rows = keep.tile([P, PACK, BANK], BF16, name="rows%d%d" % (h, b) if h + b else "wg_raw00", align_bytes=256)
-            width = BANK // 2 if (h, b) == (0, 1) else BANK
+            rows = keep.tile([P, PACK, BANK], BF16, name="rows%d%d" % (h, b), align_bytes=256)
+            width = BANK if h + b else BANK // 2
             for first in range(0, BANK, width):
                 for t in range(PACK):
                     nc.scalar.activation(
                         out=rows[:, t, first : first + width],
-                        in_=accs[PACK * b + t][:, first : first + width],
+                        in_=accs[PACK * b + t][:] if h + b else opening_scores(t, first // width),
                         func=ACT.Exp,
-                        bias=log_decay[h, b][:, t : t + 1] if h + b + t else opening_bias[:],
+                        bias=log_decay[h, b][:, t : t + 1] if h + b + t + first else opening_bias[:],
                     )
             return rows
 
@@ -208,46 +218,66 @@ def tile_list_decayed_key_read_kernel(
             return grouped
 
         def quantize_wg(b, c, grouped):
-            wg_codes[b, c] = keep.tile([P, N // 2], U32, name="wg_codes11" if c else "rows01", align_bytes=256)
+            wg_codes[b, c] = keep.tile([P, N // 2], U32, name="wg_codes%d%d" % (b, c), align_bytes=256)
             quantize(wg_codes[b, c][:], wg_plane[:, b, c * N // 2 : (c + 1) * N // 2], grouped[:])
 
         def quantize_p(h, b, grouped):
-            quantize(p_codes[h][:, b, :], p_plane[h][:, b, :], grouped[:])
+            quantize(p_codes[h, b][:], p_plane[h][:, b, :], grouped[:])
 
         wg_first = keep.tile([P, N, PACK], BF16, name="wg_first", align_bytes=256)
-        interleave(nc.scalar.copy, wg_first[:, :HEAD, :], wg_raw[0, 0][:])
-        for n in range(8):
-            score_pass(scores[n], 1, n, 0)
+        nc.gpsimd.tensor_scalar(
+            out=wg_first[:, :HEAD, :],
+            in0=wg_raw[0, 0][:].rearrange("p t n -> p n t"),
+            scalar1=1.0,
+            scalar2=0.0,
+            op0=ALU.mult,
+            op1=ALU.add,
+        )
+        for c in range(2):
+            for n in range(PACK):
+                score_pass(opening_scores(n, c), 1, n, 0, c * QUARTER, (c + 1) * QUARTER, False, n % 2 == 1)
+        for n in range(PACK, 2 * PACK):
+            score_pass(scores[n][:], 1, n, 0, 0, BANK, False, True)
         rows = {}
         for b in range(2):
             rows[0, b] = exponentials(scores, 0, b)
         scores = [bank(n) for n in range(8)]
         for n in range(8):
-            score_pass(scores[n], 0, n, 1)
-            score_pass(scores[n], 1, n, 1, 0, LATE - BANK)
-            score_pass(scores[n], 1, n, 1, LATE - BANK, BANK)
+            for a in range(2):
+                score_pass(scores[n][:], a, n, 1, 0, BANK, a == 0, a == 1)
         for b in range(2):
             rows[1, b] = exponentials(scores, 1, b)
 
+        grouped = keep.tile([P, BANK, PACK], BF16, name="p_grouped0", align_bytes=256)
+        interleave(nc.vector.tensor_copy, grouped[:, :QUARTER, :], rows[0, 0][:, :, :QUARTER])
         interleave(nc.vector.tensor_copy, wg_first[:, HEAD:, :], wg_raw[0, 1][:])
-        wg_left = group(wg_raw[1, 0][:], "wg_grouped2")
-        halves = [slice(c * BANK // 2, (c + 1) * BANK // 2) for c in range(2)]
-        grouped = group(rows[0, 0][:], "p_grouped0")
-        left = group(rows[0, 1][:, :, halves[0]], "p_left")
-        quantize_p(0, 0, grouped)
-        right = group(rows[0, 1][:, :, halves[1]], "p_right")
-        quantize(p_codes[0][:, 1, halves[0]], p_plane[0][:, 1, halves[0]], left[:])
-        quantize(p_codes[0][:, 1, halves[1]], p_plane[0][:, 1, halves[1]], right[:])
+        interleave(nc.vector.tensor_copy, grouped[:, QUARTER:, :], rows[0, 0][:, :, QUARTER:])
         first_codes = keep.tile([P, N], U32, name="first_codes", align_bytes=256)
         quantize(first_codes[:], wg_plane[:, 0, :], wg_first[:])
+        quantize_p(0, 0, grouped)
+        wg_left = group(wg_raw[1, 0][:], "wg_left")
+        grouped = group(rows[0, 1][:], "p_grouped1")
+        quantize_wg(1, 0, wg_left)
+        quantize_p(0, 1, grouped)
         for c in range(2):
             wg_codes[0, c] = first_codes[:, c * N // 2 : (c + 1) * N // 2]
-        wg_right = group(wg_raw[1, 1][:], "p_left")
-        quantize_wg(1, 0, wg_left)
-        grouped = group(rows[1, 0][:], "p_grouped2")
+        wg_right = group(wg_raw[1, 1][:], "rows01")
+        beside = OWN
+        late_groups = keep.tile([P, (beside + BANK) * PACK], BF16, name="late_groups", align_bytes=256)
+        third = late_groups[:, beside * PACK :].rearrange("p (n t) -> p n t", t=PACK)
+        fourth = late_groups[:, : BANK * PACK].rearrange("p (n t) -> p n t", t=PACK)
+        interleave(nc.vector.tensor_copy, third, rows[1, 0][:])
         quantize_wg(1, 1, wg_right)
-        quantize_p(1, 0, grouped)
-        left = group(rows[1, 1][:, :, halves[0]], "p_grouped0")
+        quantize(p_codes[1, 0][:], p_plane[1][:, 0, :], third)
+        interleave(nc.vector.tensor_copy, fourth[:, :OWN, :], rows[1, 1][:, :, :OWN])
+        nc.gpsimd.tensor_scalar(
+            out=fourth[:, beside:, :],
+            in0=rows[1, 1][:, :, beside:].rearrange("p t n -> p n t"),
+            scalar1=1.0,
+            scalar2=0.0,
+            op0=ALU.mult,
+            op1=ALU.add,
+        )
 
         def gate_pass(gate, n, h, b):
             cols = slice(n * P, (n + 1) * P)
@@ -255,7 +285,7 @@ def tile_list_decayed_key_read_kernel(
                 out=gate[:],
                 lhsT=wg_codes[b, n // 2][:, n % 2 * P : (n % 2 + 1) * P].bitcast(FP8X4),
                 lhsT_scale=wg_plane[:, b, cols],
-                rhs=p_codes[h][:, b, :].bitcast(FP8X4),
+                rhs=p_codes[h, b][:].bitcast(FP8X4),
                 rhs_scale=p_plane[h][:, b, :],
                 start=(b == 0),
                 stop=(b == 1),
@@ -267,58 +297,55 @@ def tile_list_decayed_key_read_kernel(
                 out=value[:, first:last],
                 lhsT=w4_codes[:, b, n * (P // 2) : (n + 1) * (P // 2)].bitcast(FP4X4),
                 lhsT_scale=w4_plane[:, b, :].bitcast(U8)[:, cols],
-                rhs=p_codes[h][:, b, first:last].bitcast(FP8X4),
+                rhs=p_codes[h, b][:, first:last].bitcast(FP8X4),
                 rhs_scale=p_plane[h][:, b, first:last],
                 start=(b == 0),
                 stop=(b == 1),
             )
 
-        def damping(gate, first, last):
-            damp = tail.tile([P, last - first], F32, name="damp")
+        def damping(gate, first, last, slot=None):
+            if slot:
+                damp = keep.tile([P, last - first], F32, name=slot, align_bytes=256)
+            else:
+                damp = tail.tile([P, last - first], F32, name="damp")
             nc.scalar.activation(out=damp[:], in_=gate[:, first:last], func=ACT.Tanh)
             return damp
 
         def finish(damp, value, n, h, first, last):
-            if n + h == 0:
-                result = keep.tile([P, BANK], F32, name="rows11", align_bytes=256)
-            else:
-                result = tail.tile([P, last - first], F32, name="result")
+            result = tail.tile([P, last - first], F32, name="result")
             nc.vector.scalar_tensor_tensor(
                 out=result[:], in0=damp[:], scalar=1.0, in1=value, op0=ALU.add, op1=ALU.mult
             )
             nc.sync.dma_start(out=out[n * P : (n + 1) * P, h * BANK + first : h * BANK + last], in_=result[:])
 
-        values = [bank(n) for n in range(4)]
-        gates = [bank(4 + n) for n in range(4)]
+        values = [bank(n) for n in (0, 1, 4, 5)]
+        gates = [bank(n) for n in (2, 3, 6, 7)]
         for b in range(2):
             for n in range(2):
                 value_pass(values[n], n, 0, b)
-        for read_pass, accs, first in ((value_pass, values, 2), (gate_pass, gates, 0)):
-            for n in range(first, 4):
-                for b in range(2):
-                    read_pass(accs[n], n, 0, b)
-        right = keep.tile([P, BANK // 2, PACK], BF16, name="p_right", align_bytes=256)
-        interleave(nc.scalar.copy, right[:, :SHARE, :], rows[1, 1][:, :, BANK // 2 : BANK // 2 + SHARE])
-        interleave(nc.vector.tensor_copy, right[:, SHARE:, :], rows[1, 1][:, :, BANK // 2 + SHARE :])
-        quantize(p_codes[1][:, 1, halves[0]], p_plane[1][:, 1, halves[0]], left[:])
-        quantize(p_codes[1][:, 1, halves[1]], p_plane[1][:, 1, halves[1]], right[:])
-        for n in range(4):
+            gate_pass(gates[0], 0, 0, b)
+        for read_pass, accs, n in (
+            (gate_pass, gates, 1), (value_pass, values, 2), (value_pass, values, 3),
+            (gate_pass, gates, 2), (gate_pass, gates, 3),
+        ):
+            for b in range(2):
+                read_pass(accs[n], n, 0, b)
+        for n in range(2):
+            finish(damping(gates[n], 0, BANK, None if n else "p_codes11"), values[n][:], n, 0, 0, BANK)
+        p_codes[1, 1] = keep.tile([P, BANK], U32, name="p_codes11", align_bytes=256)
+        quantize(p_codes[1, 1][:], p_plane[1][:, 1, :], fourth)
+        for n in range(2, 4):
             finish(damping(gates[n], 0, BANK), values[n][:], n, 0, 0, BANK)
-        gates = [bank(n) for n in (4, 0, 1, 2)]
-        values = [bank(n) for n in (5, 6, 7, 3)]
-        gate_pass(gates[0], 0, 1, 0)
-        value_pass(values[0], 0, 1, 0)
-        gate_pass(gates[0], 0, 1, 1)
-        value_pass(values[0], 0, 1, 1)
-        for n in range(1, 3):
-            for b in range(2):
+        gates = [bank(n) for n in (2, 0, 1, 4)]
+        values = [bank(n) for n in (3, 6, 7, 5)]
+        for b in range(2):
+            for n in range(3):
                 gate_pass(gates[n], n, 1, b)
-            for b in range(2):
                 value_pass(values[n], n, 1, b)
         finish(damping(gates[0], 0, BANK), values[0][:], 0, 1, 0, BANK)
         for b in range(2):
             gate_pass(gates[3], 3, 1, b)
-        last_values = [values[3], bank(4)]
+        last_values = [values[3], bank(2)]
         for first in range(0, BANK, P):
             for b in range(2):
                 value_pass(last_values[first // (BANK // 2)], 3, 1, b, first, first + P)

@@ -1,6 +1,7 @@
 from contextlib import ExitStack
 
 import concourse.mybir as mybir
+from concourse.masks import make_identity
 
 K, T, S, T2, S2, N = 1024, 4096, 1024, 2048, 1024, 512
 FLOPS = 2 * K * S * S2 + 2 * 2 * S * N * S2
@@ -24,7 +25,7 @@ PLANE_ROW = (0, 4)
 DENSE = 96
 HEAD = 192
 OWN = 256
-LATE = 768
+LATE = 896
 
 
 def tile_list_decayed_key_read_kernel(
@@ -51,15 +52,18 @@ def tile_list_decayed_key_read_kernel(
             (b, c): keep.tile([P, PACK, last - first], F32, name="wg_raw%d%d" % (b, c), align_bytes=256)
             for (b, c), (first, last) in wg_cuts.items()
         }
-        decay = keep.tile([P, 2, PACK], F32, name="decay")
+        decay_rows = keep.tile([P, PASS], F32, name="decay_rows")
+        identity = keep.tile([P, P], F32, name="identity")
         slots = {(0, 0): "wg_left", (0, 1): "wg_codes10", (1, 0): "wg_codes11", (1, 1): "last_bias"}
         log_decay = {hb: keep.tile([P, PACK], F32, name=slot, align_bytes=256) for hb, slot in slots.items()}
 
         planes = [keep.tile([P, (S + S2) // 4], I32, name="planes%d" % a, align_bytes=256) for a in range(2)]
         nc.vector.memset(query_scale_table[0:DENSE, :], 0)
         nc.vector.memset(key_scale_table[0:DENSE, :], 0)
+        nc.gpsimd.memset(decay_rows[:], 0.0)
         nc.gpsimd.memset(planes[0][:], 0)
         nc.gpsimd.memset(planes[1][:], 0)
+        make_identity(nc, identity[:])
         nc.gpsimd.memset(w4_plane[:], 0)
 
         def load_words(tile, words, cols):
@@ -78,7 +82,11 @@ def tile_list_decayed_key_read_kernel(
         load_key_half(0, 0)
         load_key_half(0, 1)
         load_words(query_table[0], tab2_words[0], slice(0, T2))
-        nc.scalar.dma_start(out=decay[:], in_=dec.rearrange("(b p t) -> p b t", b=2, t=PACK))
+        nc.scalar.dma_start(out=decay_rows[0:2, :], in_=dec.rearrange("(b i) -> b i", b=2))
+        turned = psum.tile([P, BANK], F32, name="bank7")
+        for t in range(PACK):
+            nc.tensor.transpose(turned[:, t * P : (t + 1) * P], decay_rows[:, t:PASS:PACK], identity[:])
+        decay = turned[:].rearrange("p (t b) -> p b t", t=PACK)
 
         for h in range(2):
             for b in range(2):

@@ -93,8 +93,6 @@ def tile_list_decayed_key_read_kernel(
                 nc.scalar.activation(out=log_decay[h, b][:], in_=decay[:, b, :], func=ACT.Ln, scale=0.5)
         opening_bias = keep.tile([P, 1], F32, name="rows01", align_bytes=256)
         nc.scalar.activation(out=opening_bias[:], in_=decay[:, 0, 0:1], func=ACT.Ln, scale=0.5)
-        warm = keep.tile([P, 1], F32, name="warm")
-        nc.scalar.activation(out=warm[:], in_=opening_bias[:], func=ACT.Exp)
 
         keys = [keep.tile([P, S], U32, name="keys%d" % a, align_bytes=256) for a in range(2)]
         queries = {}

@@ -149,13 +149,13 @@ def tile_list_decayed_key_read_kernel(
         load_wg(0, 0)
         load_wg(0, 1)
         load_wg(1, 0)
-        nc.sync.dma_start(out=w4_codes[:], in_=w4_words.bitcast(I32).rearrange("a p c -> p a c"))
-        for q in range(4):
-            nc.sync.dma_start(
-                out=w4_plane[32 * q : 32 * q + 4, :, :],
-                in_=w4_scales.bitcast(I32)[:, 4 * q : 4 * q + 4, :].rearrange("a r n -> r a n"),
-            )
         load_wg(1, 1)
+        nc.sync.dma_start(out=w4_codes[:], in_=w4_words.bitcast(I32).rearrange("a p c -> p a c"))
+        for r in range(4):
+            nc.sync.dma_start(
+                out=w4_plane[r:P:32, :, :],
+                in_=w4_scales.bitcast(I32)[:, r:16:4, :].rearrange("a q n -> q a n"),
+            )
 
         for b in range(2):
             gather_keys(0, b)
@@ -324,14 +324,14 @@ def tile_list_decayed_key_read_kernel(
             )
             nc.sync.dma_start(out=out[n * P : (n + 1) * P, h * BANK + first : h * BANK + last], in_=result[:])
 
-        values = [bank(n) for n in (0, 1, 4, 5)]
-        gates = [bank(n) for n in (2, 3, 6, 7)]
+        values = [bank(n) for n in (2, 3, 4, 5)]
+        gates = [bank(n) for n in (0, 1, 6, 7)]
         for b in range(2):
             for n in range(2):
-                value_pass(values[n], n, 0, b)
-            gate_pass(gates[0], 0, 0, b)
+                gate_pass(gates[n], n, 0, b)
+            value_pass(values[0], 0, 0, b)
         for read_pass, accs, n in (
-            (gate_pass, gates, 1), (value_pass, values, 2), (value_pass, values, 3),
+            (value_pass, values, 1), (value_pass, values, 2), (value_pass, values, 3),
             (gate_pass, gates, 2), (gate_pass, gates, 3),
         ):
             for b in range(2):
@@ -342,8 +342,8 @@ def tile_list_decayed_key_read_kernel(
         quantize(p_codes[1, 1][:], p_plane[1][:, 1, :], fourth)
         for n in range(2, 4):
             finish(damping(gates[n], 0, BANK), values[n][:], n, 0, 0, BANK)
-        gates = [bank(n) for n in (2, 0, 1, 4)]
-        values = [bank(n) for n in (3, 6, 7, 5)]
+        gates = [bank(n) for n in (0, 2, 3, 4)]
+        values = [bank(n) for n in (1, 6, 7, 5)]
         for b in range(2):
             for n in range(3):
                 gate_pass(gates[n], n, 1, b)
@@ -351,7 +351,7 @@ def tile_list_decayed_key_read_kernel(
         finish(damping(gates[0], 0, BANK), values[0][:], 0, 1, 0, BANK)
         for b in range(2):
             gate_pass(gates[3], 3, 1, b)
-        last_values = [values[3], bank(2)]
+        last_values = [values[3], bank(0)]
         for first in range(0, BANK, P):
             for b in range(2):
                 value_pass(last_values[first // (BANK // 2)], 3, 1, b, first, first + P)

from contextlib import ExitStack

import concourse.mybir as mybir
from concourse.masks import make_identity

K, T, S, T2, S2, N = 1024, 4096, 1024, 2048, 1024, 512
FLOPS = 2 * K * S * S2 + 2 * 2 * S * N * S2

F32 = mybir.dt.float32
BF16 = mybir.dt.bfloat16
I32 = mybir.dt.int32
U32 = mybir.dt.uint32
U16 = mybir.dt.uint16
U8 = mybir.dt.uint8
FP8X4 = mybir.dt.float8_e4m3fn_x4
FP4X4 = mybir.dt.float4_e2m1fn_x4
ACT = mybir.ActivationFunctionType
ALU = mybir.AluOpType

P = 128
PACK = 4
PASS = P * PACK
BANK = 512
PLANE_ROW = (0, 4)
DENSE = 96
HEAD = 192
OWN = 256
LATE = 896


def tile_list_decayed_key_read_kernel(
    tc, tab_words, tab_scales, tab2_words, tab2_scales, w4_words, w4_scales, wg, dec, offs, offs2, out
):
    nc = tc.nc
    with ExitStack() as ctx:
        lists = ctx.enter_context(tc.tile_pool(name="lists", bufs=1))
        keep = ctx.enter_context(tc.tile_pool(name="keep", bufs=1))
        tail = ctx.enter_context(tc.tile_pool(name="tail", bufs=8))
        psum = ctx.enter_context(tc.psum_pool(name="psum", bufs=1))

        key_list = lists.tile([P, S // 16], U16, name="key_list")
        query_list = lists.tile([P, S2 // 16], U16, name="query_list")

        key_table = [keep.tile([P, T], I32, name="key_table%d" % a, align_bytes=256) for a in range(2)]
        query_table = [keep.tile([P, T2], I32, name="query_table%d" % a, align_bytes=256) for a in range(2)]
        key_scale_table = keep.tile([P, T // 4], I32, name="key_scale_table", align_bytes=256)
        query_scale_table = keep.tile([P, T2 // 4], I32, name="query_scale_table", align_bytes=256)
        w4_codes = keep.tile([P, 2, N // 2], I32, name="w4_codes", align_bytes=256)
        w4_plane = keep.tile([P, 2, N // 4], I32, name="w4_plane", align_bytes=256)
        wg_cuts = {(0, 0): (0, HEAD), (0, 1): (HEAD, N), (1, 0): (0, N // 2), (1, 1): (N // 2, N)}
        wg_raw = {
            (b, c): keep.tile([P, PACK, last - first], F32, name="wg_raw%d%d" % (b, c), align_bytes=256)
            for (b, c), (first, last) in wg_cuts.items()
        }
        decay_rows = keep.tile([P, PASS], F32, name="decay_rows")
        identity = keep.tile([P, P], F32, name="identity")
        slots = {(0, 0): "wg_left", (0, 1): "wg_codes10", (1, 0): "wg_codes11", (1, 1): "last_bias"}
        log_decay = {hb: keep.tile([P, PACK], F32, name=slot, align_bytes=256) for hb, slot in slots.items()}

        planes = [keep.tile([P, (S + S2) // 4], I32, name="planes%d" % a, align_bytes=256) for a in range(2)]
        nc.vector.memset(query_scale_table[0:DENSE, :], 0)
        nc.vector.memset(key_scale_table[0:DENSE, :], 0)
        nc.gpsimd.memset(decay_rows[:], 0.0)
        nc.gpsimd.memset(planes[0][:], 0)
        nc.gpsimd.memset(planes[1][:], 0)
        make_identity(nc, identity[:])
        nc.gpsimd.memset(w4_plane[:], 0)

        def load_words(tile, words, cols):
            nc.sync.dma_start(out=tile[:, cols], in_=words.rearrange("p t i -> p (t i)").bitcast(I32)[:, cols])

        def load_key_half(a, c):
            load_words(key_table[a], tab_words[a], slice(c * T // 2, (c + 1) * T // 2))

        def load_scale_rows(tile, scales):
            nc.sync.dma_start(out=tile[DENSE:P, :], in_=scales.bitcast(I32).rearrange("a q t -> (a q) t"))

        load_scale_rows(query_scale_table, tab2_scales)
        nc.sync.dma_start(query_list[:], offs2)
        load_scale_rows(key_scale_table, tab_scales)
        nc.sync.dma_start(key_list[:], offs)
        load_key_half(0, 0)
        load_key_half(0, 1)
        load_words(query_table[0], tab2_words[0], slice(0, T2))
        nc.scalar.dma_start(out=decay_rows[0:2, :], in_=dec.rearrange("(b i) -> b i", b=2))
        turned = psum.tile([P, BANK], F32, name="bank7")
        for t in range(PACK):
            nc.tensor.transpose(turned[:, t * P : (t + 1) * P], decay_rows[:, t:PASS:PACK], identity[:])
        decay = turned[:].rearrange("p (t b) -> p b t", t=PACK)

        for h in range(2):
            for b in range(2):
                nc.scalar.activation(out=log_decay[h, b][:], in_=decay[:, b, :], func=ACT.Ln, scale=0.5)
        opening_bias = keep.tile([P, 1], F32, name="rows01", align_bytes=256)
        nc.scalar.activation(out=opening_bias[:], in_=decay[:, 0, 0:1], func=ACT.Ln, scale=0.5)

        keys = [keep.tile([P, S], U32, name="keys%d" % a, align_bytes=256) for a in range(2)]
        queries = {}
        key_plane_listed = keep.tile([P, S], U8, name="key_plane_listed", align_bytes=256)
        query_plane_listed = keep.tile([P, S2], U8, name="query_plane_listed", align_bytes=256)
        dense_planes = keep.tile([P, S + S2], U8, name="dense_planes", align_bytes=256)

        def half(h):
            return slice(h * BANK, (h + 1) * BANK)

        def list_half(tile, h):
            return tile[:, h * (BANK // 16) : (h + 1) * (BANK // 16)]

        def gather_queries(a, cuts, slot):
            queries[a, cuts[0]] = keep.tile([P, cuts[-1] - cuts[0]], U32, name=slot, align_bytes=256)
            for first, last in zip(cuts, cuts[1:]):
                nc.vector.tensor_copy(
                    queries[a, cuts[0]][:, first - cuts[0] : last - cuts[0]],
                    query_table[a][:].bitcast(U32).indirect(query_list[:, first // 16 : last // 16]),
                )

        def gather_keys(a, b):
            nc.vector.tensor_copy(
                keys[a][:, half(b)].rearrange("p (t m) -> p m t", t=PACK),
                key_table[a][:].bitcast(U32).indirect(list_half(key_list, b)),
            )

        nc.vector.tensor_copy(query_plane_listed[:], query_scale_table[:].bitcast(U8).indirect(query_list[:]))
        nc.vector.tensor_copy(key_plane_listed[:], key_scale_table[:].bitcast(U8).indirect(key_list[:]))
        nc.vector.tensor_copy(dense_planes[:, S:].bitcast(I32), query_plane_listed[:].bitcast(I32))
        nc.vector.tensor_copy(
            dense_planes[:, :S].rearrange("p (b t m) -> p b t m", b=2, t=PACK),
            key_plane_listed[:].rearrange("p (b m t) -> p b t m", b=2, t=PACK),
        )

        def place_scale_rows(a):
            for r in range(4):
                first = DENSE + 16 * a + r
                nc.sync.dma_start(
                    out=planes[a][PLANE_ROW[a] + r : P : 32, :],
                    in_=dense_planes[first : first + 13 : 4, :].bitcast(I32),
                )

        load_key_half(1, 0)
        place_scale_rows(0)
        load_key_half(1, 1)
        load_words(query_table[1], tab2_words[1], slice(0, T2))
        place_scale_rows(1)

        def load_wg(b, c):
            rows_of_pass = wg[b * PASS : (b + 1) * PASS, :].rearrange("(p t) n -> p t n", t=PACK)
            nc.sync.dma_start(out=wg_raw[b, c][:], in_=rows_of_pass[:, :, slice(*wg_cuts[b, c])])

        load_wg(0, 0)
        load_wg(0, 1)
        load_wg(1, 0)
        load_wg(1, 1)
        nc.sync.dma_start(out=w4_codes[:], in_=w4_words.bitcast(I32).rearrange("a p c -> p a c"))
        for r in range(4):
            nc.sync.dma_start(
                out=w4_plane[r:P:32, :, :],
                in_=w4_scales.bitcast(I32)[:, r:16:4, :].rearrange("a q n -> q a n"),
            )

        for b in range(2):
            gather_keys(0, b)
        gather_queries(0, (0, LATE, S2), "queries0")
        for b in range(2):
            gather_keys(1, b)
        gather_queries(1, (0, BANK // 2, BANK, S2), "queries1")

        def bank(n):
            return psum.tile([P, BANK], F32, name="bank%d" % n)

        def score_pass(acc, a, tile_index, h, first, last, opens, closes):
            cols = slice(tile_index * P, (tile_index + 1) * P)
            nc.tensor.matmul_mx(
                out=acc,
                lhsT=keys[a][:, cols].bitcast(FP8X4),
                lhsT_scale=planes[a][PLANE_ROW[a] : P, :].bitcast(U8)[:, cols],
                rhs=queries[a, 0][:, h * BANK + first : h * BANK + last].bitcast(FP8X4),
                rhs_scale=planes[a][PLANE_ROW[a] : P, :].bitcast(U8)[:, S + h * BANK + first : S + h * BANK + last],
                start=opens,
                stop=closes,
            )

        def interleave(copy, dst, src):
            run = 4 if src.dtype == F32 else 8
            copy(out=dst.rearrange("p (c i) t -> p c t i", i=run), in_=src.rearrange("p t (c i) -> p c t i", i=run))

        def quantize(codes, plane, grouped):
            nc.vector.quantize_mx(out=codes.bitcast(FP8X4), scales=plane, in_=grouped.rearrange("p n t -> p (n t)"))

        wg_codes = {}
        wg_plane = keep.tile([P, 2, N], U8, name="wg_plane", align_bytes=256)
        p_codes = {
            hb: keep.tile([P, BANK], U32, name="p_codes%d%d" % hb, align_bytes=256) for hb in ((0, 0), (0, 1), (1, 0))
        }
        p_plane = [keep.tile([P, 2, BANK], U8, name="p_plane%d" % h, align_bytes=256) for h in range(2)]

        scores = [bank(n) for n in range(8)]
        QUARTER = BANK // 2

        def opening_scores(n, c):
            return scores[2 * c + n // 2][:, n % 2 * QUARTER : (n % 2 + 1) * QUARTER]

        for c in range(2):
            for n in range(PACK):
                score_pass(opening_scores(n, c), 0, n, 0, c * QUARTER, (c + 1) * QUARTER, n % 2 == 0, False)
        for n in range(PACK, 2 * PACK):
            score_pass(scores[n][:], 0, n, 0, 0, BANK, True, False)

        def exponentials(accs, h, b):
            rows = keep.tile([P, PACK, BANK], BF16, name="rows%d%d" % (h, b), align_bytes=256)
            width = BANK if h + b else BANK // 2
            for first in range(0, BANK, width):
                for t in range(PACK):
                    nc.scalar.activation(
                        out=rows[:, t, first : first + width],
                        in_=accs[PACK * b + t][:] if h + b else opening_scores(t, first // width),
                        func=ACT.Exp,
                        bias=log_decay[h, b][:, t : t + 1] if h + b + t + first else opening_bias[:],
                    )
            return rows

        def group(src, slot, copy=nc.vector.tensor_copy):
            grouped = keep.tile([P, src.shape[2], PACK], BF16, name=slot, align_bytes=256)
            interleave(copy, grouped[:], src)
            return grouped

        def quantize_wg(b, c, grouped):
            wg_codes[b, c] = keep.tile([P, N // 2], U32, name="wg_codes%d%d" % (b, c), align_bytes=256)
            quantize(wg_codes[b, c][:], wg_plane[:, b, c * N // 2 : (c + 1) * N // 2], grouped[:])

        def quantize_p(h, b, grouped):
            quantize(p_codes[h, b][:], p_plane[h][:, b, :], grouped[:])

        wg_first = keep.tile([P, N, PACK], BF16, name="wg_first", align_bytes=256)
        nc.gpsimd.tensor_scalar(
            out=wg_first[:, :HEAD, :],
            in0=wg_raw[0, 0][:].rearrange("p t n -> p n t"),
            scalar1=1.0,
            scalar2=0.0,
            op0=ALU.mult,
            op1=ALU.add,
        )
        for c in range(2):
            for n in range(PACK):
                score_pass(opening_scores(n, c), 1, n, 0, c * QUARTER, (c + 1) * QUARTER, False, n % 2 == 1)
        for n in range(PACK, 2 * PACK):
            score_pass(scores[n][:], 1, n, 0, 0, BANK, False, True)
        rows = {}
        for b in range(2):
            rows[0, b] = exponentials(scores, 0, b)
        scores = [bank(n) for n in range(8)]
        for n in range(8):
            for a in range(2):
                score_pass(scores[n][:], a, n, 1, 0, BANK, a == 0, a == 1)
        for b in range(2):
            rows[1, b] = exponentials(scores, 1, b)

        grouped = keep.tile([P, BANK, PACK], BF16, name="p_grouped0", align_bytes=256)
        interleave(nc.vector.tensor_copy, grouped[:, :QUARTER, :], rows[0, 0][:, :, :QUARTER])
        interleave(nc.vector.tensor_copy, wg_first[:, HEAD:, :], wg_raw[0, 1][:])
        interleave(nc.vector.tensor_copy, grouped[:, QUARTER:, :], rows[0, 0][:, :, QUARTER:])
        first_codes = keep.tile([P, N], U32, name="first_codes", align_bytes=256)
        quantize(first_codes[:], wg_plane[:, 0, :], wg_first[:])
        quantize_p(0, 0, grouped)
        wg_left = group(wg_raw[1, 0][:], "wg_left")
        grouped = group(rows[0, 1][:], "p_grouped1")
        quantize_wg(1, 0, wg_left)
        quantize_p(0, 1, grouped)
        for c in range(2):
            wg_codes[0, c] = first_codes[:, c * N // 2 : (c + 1) * N // 2]
        wg_right = group(wg_raw[1, 1][:], "rows01")
        beside = OWN
        late_groups = keep.tile([P, (beside + BANK) * PACK], BF16, name="late_groups", align_bytes=256)
        third = late_groups[:, beside * PACK :].rearrange("p (n t) -> p n t", t=PACK)
        fourth = late_groups[:, : BANK * PACK].rearrange("p (n t) -> p n t", t=PACK)
        interleave(nc.vector.tensor_copy, third, rows[1, 0][:])
        quantize_wg(1, 1, wg_right)
        quantize(p_codes[1, 0][:], p_plane[1][:, 0, :], third)
        interleave(nc.vector.tensor_copy, fourth[:, :OWN, :], rows[1, 1][:, :, :OWN])
        nc.gpsimd.tensor_scalar(
            out=fourth[:, beside:, :],
            in0=rows[1, 1][:, :, beside:].rearrange("p t n -> p n t"),
            scalar1=1.0,
            scalar2=0.0,
            op0=ALU.mult,
            op1=ALU.add,
        )

        def gate_pass(gate, n, h, b):
            cols = slice(n * P, (n + 1) * P)
            nc.tensor.matmul_mx(
                out=gate[:],
                lhsT=wg_codes[b, n // 2][:, n % 2 * P : (n % 2 + 1) * P].bitcast(FP8X4),
                lhsT_scale=wg_plane[:, b, cols],
                rhs=p_codes[h, b][:].bitcast(FP8X4),
                rhs_scale=p_plane[h][:, b, :],
                start=(b == 0),
                stop=(b == 1),
            )

        def value_pass(value, n, h, b, first=0, last=BANK):
            cols = slice(n * P, (n + 1) * P)
            nc.tensor.matmul_mx(
                out=value[:, first:last],
                lhsT=w4_codes[:, b, n * (P // 2) : (n + 1) * (P // 2)].bitcast(FP4X4),
                lhsT_scale=w4_plane[:, b, :].bitcast(U8)[:, cols],
                rhs=p_codes[h, b][:, first:last].bitcast(FP8X4),
                rhs_scale=p_plane[h][:, b, first:last],
                start=(b == 0),
                stop=(b == 1),
            )

        def damping(gate, first, last, slot=None):
            if slot:
                damp = keep.tile([P, last - first], F32, name=slot, align_bytes=256)
            else:
                damp = tail.tile([P, last - first], F32, name="damp")
            nc.scalar.activation(out=damp[:], in_=gate[:, first:last], func=ACT.Tanh)
            return damp

        def finish(damp, value, n, h, first, last):
            result = tail.tile([P, last - first], F32, name="result")
            nc.vector.scalar_tensor_tensor(
                out=result[:], in0=damp[:], scalar=1.0, in1=value, op0=ALU.add, op1=ALU.mult
            )
            nc.sync.dma_start(out=out[n * P : (n + 1) * P, h * BANK + first : h * BANK + last], in_=result[:])

        values = [bank(n) for n in (2, 3, 4, 5)]
        gates = [bank(n) for n in (0, 1, 6, 7)]
        for b in range(2):
            for n in range(2):
                gate_pass(gates[n], n, 0, b)
            value_pass(values[0], 0, 0, b)
        for read_pass, accs, n in (
            (value_pass, values, 1), (value_pass, values, 2), (value_pass, values, 3),
            (gate_pass, gates, 2), (gate_pass, gates, 3),
        ):
            for b in range(2):
                read_pass(accs[n], n, 0, b)
        for n in range(2):
            finish(damping(gates[n], 0, BANK, None if n else "p_codes11"), values[n][:], n, 0, 0, BANK)
        p_codes[1, 1] = keep.tile([P, BANK], U32, name="p_codes11", align_bytes=256)
        quantize(p_codes[1, 1][:], p_plane[1][:, 1, :], fourth)
        for n in range(2, 4):
            finish(damping(gates[n], 0, BANK), values[n][:], n, 0, 0, BANK)
        gates = [bank(n) for n in (0, 2, 3, 4)]
        values = [bank(n) for n in (1, 6, 7, 5)]
        for b in range(2):
            for n in range(3):
                gate_pass(gates[n], n, 1, b)
                value_pass(values[n], n, 1, b)
        finish(damping(gates[0], 0, BANK), values[0][:], 0, 1, 0, BANK)
        for b in range(2):
            gate_pass(gates[3], 3, 1, b)
        last_values = [values[3], bank(0)]
        for first in range(0, BANK, P):
            for b in range(2):
                value_pass(last_values[first // (BANK // 2)], 3, 1, b, first, first + P)
        for n in range(1, 3):
            finish(damping(gates[n], 0, BANK), values[n][:], n, 1, 0, BANK)
        for c in range(2):
            first, last = c * BANK // 2, (c + 1) * BANK // 2
            finish(damping(gates[3], first, last), last_values[c][:, first:last], 3, 1, first, last)
